import numpy as np
import ml_dtypes


def mxq(x, axis, fmt="e4m3"):
    dtype, down = {"e4m3": (ml_dtypes.float8_e4m3fn, 7), "e5m2": (ml_dtypes.float8_e5m2, 14)}[fmt]
    v = np.moveaxis(np.asarray(x, np.float32).astype(ml_dtypes.bfloat16).astype(np.float64), axis, -1)
    blocks = v.reshape(v.shape[:-1] + (-1, 32))
    amax = np.abs(blocks).max(-1, keepdims=True)
    byte = np.maximum(np.where(amax > 0, np.frexp(amax)[1] - 1 + 127, 0) - down, 1)
    scale = np.exp2(byte - 127.0)
    codes = (blocks / scale).astype(np.float32).astype(dtype).astype(np.float64)
    return np.moveaxis((codes * scale).reshape(v.shape), -1, axis)


WIDE = False


def mx_kscale(k):
    if not WIDE:
        return np.ones(k)
    levels = np.array([10, -10, 5, -5, 0])
    if k % 512:
        return np.exp2(np.random.permutation(np.resize(levels, k // 32))).repeat(32)
    a = np.empty((k // 512, 16))
    for p in range(k // 512):
        a[p, :8] = np.random.permutation(np.resize(levels, 8))
        for g in range(8):
            far = levels[np.abs(levels - a[p, g]) >= 10]
            a[p, g + 8] = far[np.random.randint(len(far))]
    return np.exp2(a.ravel()).repeat(32)


def f64(x):
    return np.asarray(x).astype(np.float64)


def striped(idx):
    return np.tile(idx.reshape(-1, 16).T, (8, 1)).astype(np.uint16)


def unstriped(offs):
    return offs[:16].T.reshape(-1).astype(np.int64)


def relu(v):
    return np.maximum(v, 0.0)


K, T, S, N = 512, 512, 512, 2048


def setup_inputs():
    n = np.random.standard_normal
    s = mx_kscale(K)[:, None]
    return {
        "w": (n((K, N)) / np.sqrt(K) / s).astype(np.float32),
        "xT": (n((K, T)) * s).astype(np.float32),
        "b": (0.3 * n((S, 1))).astype(np.float32),
        "offs": striped(np.sort(np.random.permutation(N)[:S])),
    }


def reference(w, xT, b, offs):
    idx = unstriped(offs)
    wq = mxq(f64(w)[:, idx], 0, "e4m3")
    return relu((wq.T @ mxq(f64(xT), 0, "e4m3")) + f64(b))

@@ -1,0 +1,137 @@
+from contextlib import ExitStack
+
+import concourse.mybir as mybir
+from concourse.masks import make_identity
+
+K, N, T, S = 512, 2048, 512, 512
+FLOPS = 2 * K * S * T
+
+F32 = mybir.dt.float32
+BF16 = mybir.dt.bfloat16
+U32 = mybir.dt.uint32
+U16 = mybir.dt.uint16
+U8 = mybir.dt.uint8
+FP8X4 = mybir.dt.float8_e4m3fn_x4
+ADD, MAX = mybir.AluOpType.add, mybir.AluOpType.max
+RELU = mybir.ActivationFunctionType.Relu
+
+P = 128
+PACK = 4
+H = 256
+FIRST = N - H
+
+
+def tile_picked_neuron_lin_relu_srt_e_kernel(tc, w, xT, b, offs, out):
+    nc = tc.nc
+    with ExitStack() as ctx:
+        keep = ctx.enter_context(tc.tile_pool(name="keep", bufs=1))
+        psum = ctx.enter_context(tc.psum_pool(name="psum", bufs=8))
+
+        w_rows = w.rearrange("(p j) n -> p j n", j=PACK)
+        x_rows = xT.rearrange("(p j) t -> p j t", j=PACK)
+
+        lists = keep.tile([P, S // 16], U16, name="lists")
+        planes = [keep.tile([P, N], F32, name="plane%d" % j) for j in range(PACK)]
+        x_raw = [keep.tile([P, PACK, T], F32, name="x_raw%d" % h) for h in range(1)]
+        b_rows = keep.tile([P, P], F32, name="b_rows")
+        ident = keep.tile([P, P], F32, name="ident")
+        bias = keep.tile([P, PACK], F32, name="bias")
+        warm = keep.tile([P, 1], F32, name="warm")
+
+        nc.vector.memset(b_rows[:], 0.0)
+        nc.vector.memset(warm[:], 0.0)
+        nc.scalar.activation(warm[:], warm[:], RELU)
+        nc.sync.dma_start(x_raw[0][:], x_rows)
+        nc.sync.dma_start(lists[:], offs)
+        nc.sync.dma_start(b_rows[0:4, :], b.rearrange("(q m) o -> q (m o)", m=P))
+        nc.sync.dma_start(planes[0][:], w_rows[:, 0, :])
+        nc.sync.dma_start(planes[1][:], w_rows[:, 1, :])
+        nc.sync.dma_start(planes[2][:], w_rows[:, 2, :])
+        nc.sync.dma_start(planes[3][:, 0:FIRST], w_rows[:, 3, 0:FIRST])
+        nc.sync.dma_start(planes[3][:, FIRST:N], w_rows[:, 3, FIRST:N])
+
+        make_identity(nc, ident[:])
+        b_bank = psum.tile([P, P], F32, name="b_bank", tag="bank")
+        nc.tensor.transpose(b_bank[:], b_rows[:], ident[:])
+        nc.scalar.copy(bias[:], b_bank[:, 0:PACK])
+
+        picked = keep.tile([P, 2, S], F32, name="picked")
+        grouped = [keep.tile([P, H, PACK], BF16, name="grouped%d" % h, align_bytes=64) for h in range(2)]
+        codes = [keep.tile([P, H], U32, name="codes%d" % h, align_bytes=64) for h in range(2)]
+        scales = [keep.tile([P, H], U8, name="scales%d" % h, align_bytes=64) for h in range(2)]
+        x_grouped = keep.tile([P, T, PACK], BF16, name="x_grouped", align_bytes=64)
+        x_codes = keep.tile([P, T], U32, name="x_codes", align_bytes=64)
+        x_scales = keep.tile([P, T], U8, name="x_scales", align_bytes=64)
+
+        def weave(copy, h, j0):
+            cols = slice(h * H, (h + 1) * H)
+            copy(out=grouped[h][:, :, j0 : j0 + 2], in_=picked[:, j0 : j0 + 2, cols].rearrange("p j n -> p n j"))
+
+        def weave_x(copy, h, lo, hi):
+            copy(out=x_grouped[:, lo:hi, :], in_=x_raw[h][:, :, lo:hi].rearrange("p j n -> p n j"))
+
+        def quantise(codes_t, scales_t, grouped_t):
+            nc.vector.quantize_mx(
+                out=codes_t.bitcast(FP8X4), scales=scales_t, in_=grouped_t.rearrange("p n j -> p (n j)")
+            )
+
+        def quantise_x(lo, hi):
+            quantise(x_codes[:, lo:hi], x_scales[:, lo:hi], x_grouped[:, lo:hi, :])
+
+        def quantise_w(h):
+            quantise(codes[h][:], scales[h][:], grouped[h][:])
+
+        def multiply(q, lo, hi):
+            acc = psum.tile([P, hi - lo], F32, name="acc", tag="bank")
+            cols = slice((q % 2) * P, (q % 2 + 1) * P)
+            nc.tensor.matmul_mx(
+                out=acc[:],
+                lhsT=codes[q // 2][:, cols].bitcast(FP8X4),
+                lhsT_scale=scales[q // 2][:, cols],
+                rhs=x_codes[:, lo:hi].bitcast(FP8X4),
+                rhs_scale=x_scales[:, lo:hi],
+                start=True,
+                stop=True,
+            )
+            return acc
+
+        results = [keep.tile([P, T], F32, name="result%d" % q) for q in range(4)]
+
+        def finish_scalar(acc, q, lo, hi):
+            nc.scalar.activation(results[q][:, lo:hi], acc[:], RELU, bias=bias[:, q : q + 1])
+
+        def finish_vector(acc, q, lo, hi):
+            nc.vector.tensor_scalar(results[q][:, lo:hi], acc[:], bias[:, q : q + 1], 0.0, op0=ADD, op1=MAX)
+
+        def store(q):
+            nc.sync.dma_start(out[q * P : (q + 1) * P, :], results[q][:])
+
+        scrap = psum.tile([P, P], F32, name="scrap", tag="bank")
+
+        def exercise(j, count):
+            for i in range(count):
+                nc.tensor.transpose(scrap[:], planes[j][:, i * P : (i + 1) * P], ident[:])
+
+        weave_x(nc.scalar.copy, 0, 0, T)
+        quantise_x(0, T)
+        for j in range(2):
+            nc.vector.tensor_copy(picked[:, j, :], planes[j][:].indirect(lists[:]))
+        weave(nc.scalar.copy, 0, 0)
+        weave(nc.scalar.copy, 1, 0)
+        for h in range(2):
+            nc.vector.tensor_copy(grouped[h][:, :, 2], planes[2][:].indirect(lists[:, h * H // 16 : (h + 1) * H // 16]))
+        exercise(2, 16)
+        nc.vector.tensor_copy(grouped[0][:, :, 3], planes[3][:, 0:FIRST].indirect(lists[:, 0 : H // 16]))
+        exercise(3, 6)
+        quantise_w(0)
+        for h in range(2):
+            acc = multiply(0, h * H, (h + 1) * H)
+            finish_scalar(acc, 0, h * H, (h + 1) * H)
+            nc.sync.dma_start(out[0:P, h * H : (h + 1) * H], results[0][:, h * H : (h + 1) * H])
+        nc.vector.tensor_copy(grouped[1][:, :, 3], planes[3][:].indirect(lists[:, H // 16 : S // 16]))
+        quantise_w(1)
+        for q in range(1, 4):
+            for h in range(2):
+                acc = multiply(q, h * H, (h + 1) * H)
+                (finish_scalar, finish_vector)[h](acc, q, h * H, (h + 1) * H)
+            store(q)

@@ -1,7 +1,6 @@
 from contextlib import ExitStack
 
 import concourse.mybir as mybir
-from concourse.masks import make_identity
 
 K, N, T, S = 512, 2048, 512, 512
 FLOPS = 2 * K * S * T
@@ -33,27 +32,20 @@ def tile_picked_neuron_lin_relu_srt_e_kernel(tc, w, xT, b, offs, out):
         lists = keep.tile([P, S // 16], U16, name="lists")
         planes = [keep.tile([P, N], F32, name="plane%d" % j) for j in range(PACK)]
         x_raw = [keep.tile([P, PACK, T], F32, name="x_raw%d" % h) for h in range(1)]
-        b_rows = keep.tile([P, P], F32, name="b_rows")
-        ident = keep.tile([P, P], F32, name="ident")
         bias = keep.tile([P, PACK], F32, name="bias")
         warm = keep.tile([P, 1], F32, name="warm")
 
-        nc.vector.memset(b_rows[:], 0.0)
         nc.vector.memset(warm[:], 0.0)
         nc.scalar.activation(warm[:], warm[:], RELU)
-        nc.sync.dma_start(x_raw[0][:], x_rows)
-        nc.sync.dma_start(lists[:], offs)
-        nc.sync.dma_start(b_rows[0:4, :], b.rearrange("(q m) o -> q (m o)", m=P))
         nc.sync.dma_start(planes[0][:], w_rows[:, 0, :])
+        nc.sync.dma_start(lists[:], offs)
         nc.sync.dma_start(planes[1][:], w_rows[:, 1, :])
+        nc.sync.dma_start(x_raw[0][:], x_rows)
         nc.sync.dma_start(planes[2][:], w_rows[:, 2, :])
         nc.sync.dma_start(planes[3][:, 0:FIRST], w_rows[:, 3, 0:FIRST])
         nc.sync.dma_start(planes[3][:, FIRST:N], w_rows[:, 3, FIRST:N])
-
-        make_identity(nc, ident[:])
-        b_bank = psum.tile([P, P], F32, name="b_bank", tag="bank")
-        nc.tensor.transpose(b_bank[:], b_rows[:], ident[:])
-        nc.scalar.copy(bias[:], b_bank[:, 0:PACK])
+        with nc.allow_non_contiguous_dma(reason="one bias value a partition"):
+            nc.sync.dma_start(bias[:], b.rearrange("(q p) o -> p (q o)", p=P))
 
         picked = keep.tile([P, 2, S], F32, name="picked")
         grouped = [keep.tile([P, H, PACK], BF16, name="grouped%d" % h, align_bytes=64) for h in range(2)]
@@ -106,23 +98,31 @@ def tile_picked_neuron_lin_relu_srt_e_kernel(tc, w, xT, b, offs, out):
         def store(q):
             nc.sync.dma_start(out[q * P : (q + 1) * P, :], results[q][:])
 
-        scrap = psum.tile([P, P], F32, name="scrap", tag="bank")
+        scrap = psum.tile([32, T], F32, name="scrap", tag="bank")
 
-        def exercise(j, count):
+        def exercise(count):
             for i in range(count):
-                nc.tensor.transpose(scrap[:], planes[j][:, i * P : (i + 1) * P], ident[:])
+                nc.tensor.matmul_mx(
+                    out=scrap[:],
+                    lhsT=x_codes[:, 0:32].bitcast(FP8X4),
+                    lhsT_scale=x_scales[:, 0:32],
+                    rhs=x_codes[:].bitcast(FP8X4),
+                    rhs_scale=x_scales[:],
+                    start=True,
+                    stop=True,
+                )
 
-        weave_x(nc.scalar.copy, 0, 0, T)
-        quantise_x(0, T)
         for j in range(2):
             nc.vector.tensor_copy(picked[:, j, :], planes[j][:].indirect(lists[:]))
         weave(nc.scalar.copy, 0, 0)
         weave(nc.scalar.copy, 1, 0)
+        weave_x(nc.scalar.copy, 0, 0, H)
+        weave_x(nc.vector.tensor_copy, 0, H, T)
+        quantise_x(0, T)
+        exercise(4)
         for h in range(2):
             nc.vector.tensor_copy(grouped[h][:, :, 2], planes[2][:].indirect(lists[:, h * H // 16 : (h + 1) * H // 16]))
-        exercise(2, 16)
         nc.vector.tensor_copy(grouped[0][:, :, 3], planes[3][:, 0:FIRST].indirect(lists[:, 0 : H // 16]))
-        exercise(3, 6)
         quantise_w(0)
         for h in range(2):
             acc = multiply(0, h * H, (h + 1) * H)

@@ -70,8 +70,9 @@ def tile_picked_neuron_lin_relu_srt_e_kernel(tc, w, xT, b, offs, out):
         def quantise_x(lo, hi):
             quantise(x_codes[:, lo:hi], x_scales[:, lo:hi], x_grouped[:, lo:hi, :])
 
-        def quantise_w(h):
-            quantise(codes[h][:], scales[h][:], grouped[h][:])
+        def quantise_w(q):
+            cols = slice((q % 2) * P, (q % 2 + 1) * P)
+            quantise(codes[q // 2][:, cols], scales[q // 2][:, cols], grouped[q // 2][:, cols, :])
 
         def multiply(q, lo, hi):
             acc = psum.tile([P, hi - lo], F32, name="acc", tag="bank")
@@ -97,6 +98,9 @@ def tile_picked_neuron_lin_relu_srt_e_kernel(tc, w, xT, b, offs, out):
 
         def store(q):
             nc.sync.dma_start(out[q * P : (q + 1) * P, :], results[q][:])
+
+        def store_half(q, h):
+            nc.sync.dma_start(out[q * P : (q + 1) * P, h * H : (h + 1) * H], results[q][:, h * H : (h + 1) * H])
 
         scrap = psum.tile([32, T], F32, name="scrap", tag="bank")
 
@@ -124,14 +128,19 @@ def tile_picked_neuron_lin_relu_srt_e_kernel(tc, w, xT, b, offs, out):
             nc.vector.tensor_copy(grouped[h][:, :, 2], planes[2][:].indirect(lists[:, h * H // 16 : (h + 1) * H // 16]))
         nc.vector.tensor_copy(grouped[0][:, :, 3], planes[3][:, 0:FIRST].indirect(lists[:, 0 : H // 16]))
         quantise_w(0)
-        for h in range(2):
-            acc = multiply(0, h * H, (h + 1) * H)
-            finish_scalar(acc, 0, h * H, (h + 1) * H)
-            nc.sync.dma_start(out[0:P, h * H : (h + 1) * H], results[0][:, h * H : (h + 1) * H])
-        nc.vector.tensor_copy(grouped[1][:, :, 3], planes[3][:].indirect(lists[:, H // 16 : S // 16]))
         quantise_w(1)
-        for q in range(1, 4):
+        for q in range(2):
+            for h in range(2):
+                acc = multiply(q, h * H, (h + 1) * H)
+                finish_scalar(acc, q, h * H, (h + 1) * H)
+                store_half(q, h)
+        nc.vector.tensor_copy(grouped[1][:, :, 3], planes[3][:].indirect(lists[:, H // 16 : S // 16]))
+        quantise_w(2)
+        quantise_w(3)
+        for q in range(2, 4):
             for h in range(2):
                 acc = multiply(q, h * H, (h + 1) * H)
                 (finish_scalar, finish_vector)[h](acc, q, h * H, (h + 1) * H)
-            store(q)
+                if q == 2:
+                    store_half(q, h)
+        store(3)

@@ -31,87 +31,92 @@ def tile_picked_neuron_lin_relu_srt_e_kernel(tc, w, xT, b, offs, out):
 
         lists = keep.tile([P, S // 16], U16, name="lists")
         planes = [keep.tile([P, N], F32, name="plane%d" % j) for j in range(PACK)]
-        x_raw = [keep.tile([P, PACK, T], F32, name="x_raw%d" % h) for h in range(1)]
-        bias = keep.tile([P, PACK], F32, name="bias")
+        x_raw = [keep.tile([P, PACK, H], F32, name="x_raw%d" % h, tag="x_raw%d" % h) for h in range(2)]
+        b_rows = keep.tile([P, P], F32, name="b_rows", align_bytes=64)
+        bias = keep.tile([P, P], F32, name="bias", align_bytes=64)
         warm = keep.tile([P, 1], F32, name="warm")
 
+        nc.vector.memset(b_rows[:], 0.0)
         nc.vector.memset(warm[:], 0.0)
         nc.scalar.activation(warm[:], warm[:], RELU)
         nc.sync.dma_start(planes[0][:], w_rows[:, 0, :])
         nc.sync.dma_start(lists[:], offs)
+        nc.sync.dma_start(
+            b_rows[0:P:32, :].rearrange("r (q i) -> r q i", i=32), b.rearrange("(q r i) o -> r q (i o)", r=4, i=32)
+        )
         nc.sync.dma_start(planes[1][:], w_rows[:, 1, :])
-        nc.sync.dma_start(x_raw[0][:], x_rows)
         nc.sync.dma_start(planes[2][:], w_rows[:, 2, :])
         nc.sync.dma_start(planes[3][:, 0:FIRST], w_rows[:, 3, 0:FIRST])
+        nc.sync.dma_start(x_raw[0][:], x_rows[:, :, 0:H])
         nc.sync.dma_start(planes[3][:, FIRST:N], w_rows[:, 3, FIRST:N])
-        with nc.allow_non_contiguous_dma(reason="one bias value a partition"):
-            nc.sync.dma_start(bias[:], b.rearrange("(q p) o -> p (q o)", p=P))
+        nc.sync.dma_start(x_raw[1][:], x_rows[:, :, H:T])
+        nc.vector.transpose(bias[:], b_rows[:])
 
         picked = keep.tile([P, 2, S], F32, name="picked")
         grouped = [keep.tile([P, H, PACK], BF16, name="grouped%d" % h, align_bytes=64) for h in range(2)]
-        codes = [keep.tile([P, H], U32, name="codes%d" % h, align_bytes=64) for h in range(2)]
+        codes = [keep.tile([P, H], U32, name="codes0", align_bytes=64)]
         scales = [keep.tile([P, H], U8, name="scales%d" % h, align_bytes=64) for h in range(2)]
-        x_grouped = keep.tile([P, T, PACK], BF16, name="x_grouped", align_bytes=64)
-        x_codes = keep.tile([P, T], U32, name="x_codes", align_bytes=64)
-        x_scales = keep.tile([P, T], U8, name="x_scales", align_bytes=64)
+        x_grouped = [keep.tile([P, H, PACK], BF16, name="x_grouped%d" % h, tag="x_grouped%d" % h, align_bytes=64) for h in range(2)]
+        x_codes = [keep.tile([P, H], U32, name="x_codes%d" % h, align_bytes=64) for h in range(2)]
+        x_scales = [keep.tile([P, H], U8, name="x_scales%d" % h, align_bytes=64) for h in range(2)]
 
         def weave(copy, h, j0):
             cols = slice(h * H, (h + 1) * H)
             copy(out=grouped[h][:, :, j0 : j0 + 2], in_=picked[:, j0 : j0 + 2, cols].rearrange("p j n -> p n j"))
 
         def weave_x(copy, h, lo, hi):
-            copy(out=x_grouped[:, lo:hi, :], in_=x_raw[h][:, :, lo:hi].rearrange("p j n -> p n j"))
+            copy(out=x_grouped[h][:, lo:hi, :], in_=x_raw[h][:, :, lo:hi].rearrange("p j n -> p n j"))
 
         def quantise(codes_t, scales_t, grouped_t):
             nc.vector.quantize_mx(
                 out=codes_t.bitcast(FP8X4), scales=scales_t, in_=grouped_t.rearrange("p n j -> p (n j)")
             )
 
-        def quantise_x(lo, hi):
-            quantise(x_codes[:, lo:hi], x_scales[:, lo:hi], x_grouped[:, lo:hi, :])
+        def quantise_x(h, lo, hi):
+            quantise(x_codes[h][:, lo:hi], x_scales[h][:, lo:hi], x_grouped[h][:, lo:hi, :])
 
-        def quantise_w(q):
-            cols = slice((q % 2) * P, (q % 2 + 1) * P)
-            quantise(codes[q // 2][:, cols], scales[q // 2][:, cols], grouped[q // 2][:, cols, :])
+        def quantise_w(h, lo, hi):
+            quantise(codes[h][:, lo:hi], scales[h][:, lo:hi], grouped[h][:, lo:hi, :])
 
-        def multiply(q, lo, hi):
-            acc = psum.tile([P, hi - lo], F32, name="acc", tag="bank")
+        def multiply(q, h):
+            acc = psum.tile([P, H], F32, name="acc", tag="bank")
             cols = slice((q % 2) * P, (q % 2 + 1) * P)
             nc.tensor.matmul_mx(
                 out=acc[:],
                 lhsT=codes[q // 2][:, cols].bitcast(FP8X4),
                 lhsT_scale=scales[q // 2][:, cols],
-                rhs=x_codes[:, lo:hi].bitcast(FP8X4),
-                rhs_scale=x_scales[:, lo:hi],
+                rhs=x_codes[h][:].bitcast(FP8X4),
+                rhs_scale=x_scales[h][:],
                 start=True,
                 stop=True,
             )
             return acc
 
-        results = [keep.tile([P, T], F32, name="result%d" % q) for q in range(4)]
+        results = [[keep.tile([P, H], F32, name="result%d_%d" % (q, h)) for h in range(2)] for q in range(4)]
 
-        def finish_scalar(acc, q, lo, hi):
-            nc.scalar.activation(results[q][:, lo:hi], acc[:], RELU, bias=bias[:, q : q + 1])
+        def finish_scalar(q, h):
+            nc.scalar.activation(results[q][h][:], multiply(q, h)[:], RELU, bias=bias[:, 32 * q : 32 * q + 1])
+            nc.sync.dma_start(out[q * P : (q + 1) * P, h * H : (h + 1) * H], results[q][h][:])
 
-        def finish_vector(acc, q, lo, hi):
-            nc.vector.tensor_scalar(results[q][:, lo:hi], acc[:], bias[:, q : q + 1], 0.0, op0=ADD, op1=MAX)
+        def finish_vector(q, h):
+            nc.vector.tensor_scalar(
+                results[q][h][:], multiply(q, h)[:], bias[:, 32 * q : 32 * q + 1], 0.0, op0=ADD, op1=MAX
+            )
+            nc.sync.dma_start(out[q * P : (q + 1) * P, h * H : (h + 1) * H], results[q][h][:])
 
-        def store(q):
-            nc.sync.dma_start(out[q * P : (q + 1) * P, :], results[q][:])
+        def gather(h, j, window):
+            nc.vector.tensor_copy(grouped[h][:, :, j], window.indirect(lists[:, h * H // 16 : (h + 1) * H // 16]))
 
-        def store_half(q, h):
-            nc.sync.dma_start(out[q * P : (q + 1) * P, h * H : (h + 1) * H], results[q][:, h * H : (h + 1) * H])
-
-        scrap = psum.tile([32, T], F32, name="scrap", tag="bank")
+        scrap = psum.tile([32, P], F32, name="scrap", tag="bank")
 
         def exercise(count):
             for i in range(count):
                 nc.tensor.matmul_mx(
                     out=scrap[:],
-                    lhsT=x_codes[:, 0:32].bitcast(FP8X4),
-                    lhsT_scale=x_scales[:, 0:32],
-                    rhs=x_codes[:].bitcast(FP8X4),
-                    rhs_scale=x_scales[:],
+                    lhsT=codes[0][:, 0:32].bitcast(FP8X4),
+                    lhsT_scale=scales[0][:, 0:32],
+                    rhs=codes[0][:, 0:P].bitcast(FP8X4),
+                    rhs_scale=scales[0][:, 0:P],
                     start=True,
                     stop=True,
                 )
@@ -120,27 +125,23 @@ def tile_picked_neuron_lin_relu_srt_e_kernel(tc, w, xT, b, offs, out):
             nc.vector.tensor_copy(picked[:, j, :], planes[j][:].indirect(lists[:]))
         weave(nc.scalar.copy, 0, 0)
         weave(nc.scalar.copy, 1, 0)
-        weave_x(nc.scalar.copy, 0, 0, H)
-        weave_x(nc.vector.tensor_copy, 0, H, T)
-        quantise_x(0, T)
-        exercise(4)
         for h in range(2):
-            nc.vector.tensor_copy(grouped[h][:, :, 2], planes[2][:].indirect(lists[:, h * H // 16 : (h + 1) * H // 16]))
-        nc.vector.tensor_copy(grouped[0][:, :, 3], planes[3][:, 0:FIRST].indirect(lists[:, 0 : H // 16]))
-        quantise_w(0)
-        quantise_w(1)
-        for q in range(2):
-            for h in range(2):
-                acc = multiply(q, h * H, (h + 1) * H)
-                finish_scalar(acc, q, h * H, (h + 1) * H)
-                store_half(q, h)
-        nc.vector.tensor_copy(grouped[1][:, :, 3], planes[3][:].indirect(lists[:, H // 16 : S // 16]))
-        quantise_w(2)
-        quantise_w(3)
-        for q in range(2, 4):
-            for h in range(2):
-                acc = multiply(q, h * H, (h + 1) * H)
-                (finish_scalar, finish_vector)[h](acc, q, h * H, (h + 1) * H)
-                if q == 2:
-                    store_half(q, h)
-        store(3)
+            gather(h, 2, planes[2][:])
+        gather(0, 3, planes[3][:, 0:FIRST])
+        quantise_w(0, 0, H)
+        exercise(10)
+        weave_x(nc.scalar.copy, 0, 0, 160)
+        weave_x(nc.vector.tensor_copy, 0, 160, H)
+        gather(1, 3, planes[3][:])
+        quantise_x(0, 0, H)
+        codes.append(keep.tile([P, H], U32, name="codes1", tag="x_grouped0", align_bytes=64))
+        quantise_w(1, 0, P)
+        quantise_w(1, P, H)
+        weave_x(nc.vector.tensor_copy, 1, 0, P)
+        weave_x(nc.vector.tensor_copy, 1, P, H)
+        quantise_x(1, 0, P)
+        quantise_x(1, P, H)
+        for q in range(4):
+            finish_scalar(q, 0)
+        for q in range(4):
+            (finish_vector, finish_scalar)[q % 2](q, 1)

@@ -31,7 +31,7 @@ def tile_picked_neuron_lin_relu_srt_e_kernel(tc, w, xT, b, offs, out):
 
         lists = keep.tile([P, S // 16], U16, name="lists")
         planes = [keep.tile([P, N], F32, name="plane%d" % j) for j in range(PACK)]
-        x_raw = [keep.tile([P, PACK, H], F32, name="x_raw%d" % h, tag="x_raw%d" % h) for h in range(2)]
+        x_raw = [keep.tile([P, PACK, H], F32, name="x_raw%d" % h, tag="x_raw%d" % h, align_bytes=64) for h in range(2)]
         b_rows = keep.tile([P, P], F32, name="b_rows", align_bytes=64)
         bias = keep.tile([P, P], F32, name="bias", align_bytes=64)
         warm = keep.tile([P, 1], F32, name="warm")
@@ -78,15 +78,15 @@ def tile_picked_neuron_lin_relu_srt_e_kernel(tc, w, xT, b, offs, out):
         def quantise_w(h, lo, hi):
             quantise(codes[h][:, lo:hi], scales[h][:, lo:hi], grouped[h][:, lo:hi, :])
 
-        def multiply(q, h):
-            acc = psum.tile([P, H], F32, name="acc", tag="bank")
+        def multiply(q, h, lo, hi):
+            acc = psum.tile([P, hi - lo], F32, name="acc", tag="bank")
             cols = slice((q % 2) * P, (q % 2 + 1) * P)
             nc.tensor.matmul_mx(
                 out=acc[:],
                 lhsT=codes[q // 2][:, cols].bitcast(FP8X4),
                 lhsT_scale=scales[q // 2][:, cols],
-                rhs=x_codes[h][:].bitcast(FP8X4),
-                rhs_scale=x_scales[h][:],
+                rhs=x_codes[h][:, lo:hi].bitcast(FP8X4),
+                rhs_scale=x_scales[h][:, lo:hi],
                 start=True,
                 stop=True,
             )
@@ -94,15 +94,17 @@ def tile_picked_neuron_lin_relu_srt_e_kernel(tc, w, xT, b, offs, out):
 
         results = [[keep.tile([P, H], F32, name="result%d_%d" % (q, h)) for h in range(2)] for q in range(4)]
 
-        def finish_scalar(q, h):
-            nc.scalar.activation(results[q][h][:], multiply(q, h)[:], RELU, bias=bias[:, 32 * q : 32 * q + 1])
-            nc.sync.dma_start(out[q * P : (q + 1) * P, h * H : (h + 1) * H], results[q][h][:])
+        def finish_scalar(q, h, lo, hi):
+            result = results[q][h][:, lo:hi]
+            nc.scalar.activation(result, multiply(q, h, lo, hi)[:], RELU, bias=bias[:, 32 * q : 32 * q + 1])
+            nc.sync.dma_start(out[q * P : (q + 1) * P, h * H + lo : h * H + hi], result)
 
-        def finish_vector(q, h):
+        def finish_vector(q, h, lo, hi):
+            result = results[q][h][:, lo:hi]
             nc.vector.tensor_scalar(
-                results[q][h][:], multiply(q, h)[:], bias[:, 32 * q : 32 * q + 1], 0.0, op0=ADD, op1=MAX
+                result, multiply(q, h, lo, hi)[:], bias[:, 32 * q : 32 * q + 1], 0.0, op0=ADD, op1=MAX
             )
-            nc.sync.dma_start(out[q * P : (q + 1) * P, h * H : (h + 1) * H], results[q][h][:])
+            nc.sync.dma_start(out[q * P : (q + 1) * P, h * H + lo : h * H + hi], result)
 
         def gather(h, j, window):
             nc.vector.tensor_copy(grouped[h][:, :, j], window.indirect(lists[:, h * H // 16 : (h + 1) * H // 16]))
@@ -129,19 +131,25 @@ def tile_picked_neuron_lin_relu_srt_e_kernel(tc, w, xT, b, offs, out):
             gather(h, 2, planes[2][:])
         gather(0, 3, planes[3][:, 0:FIRST])
         quantise_w(0, 0, H)
-        exercise(10)
+        exercise(9)
         weave_x(nc.scalar.copy, 0, 0, 160)
         weave_x(nc.vector.tensor_copy, 0, 160, H)
         gather(1, 3, planes[3][:])
-        quantise_x(0, 0, H)
-        codes.append(keep.tile([P, H], U32, name="codes1", tag="x_grouped0", align_bytes=64))
+        quantise_x(0, 0, P)
+        quantise_x(0, P, H)
+        codes.append(keep.tile([P, H], U32, name="codes1", tag="x_raw0", align_bytes=64))
         quantise_w(1, 0, P)
         quantise_w(1, P, H)
         weave_x(nc.vector.tensor_copy, 1, 0, P)
         weave_x(nc.vector.tensor_copy, 1, P, H)
         quantise_x(1, 0, P)
         quantise_x(1, P, H)
-        for q in range(4):
-            finish_scalar(q, 0)
-        for q in range(4):
-            (finish_vector, finish_scalar)[q % 2](q, 1)
+        finish_scalar(0, 0, 0, P)
+        finish_scalar(0, 0, P, H)
+        for q in range(1, 4):
+            finish_scalar(q, 0, 0, H)
+        finish_scalar(0, 1, 0, P)
+        finish_vector(0, 1, P, H)
+        finish_scalar(1, 1, 0, H)
+        finish_vector(2, 1, 0, H)
+        finish_scalar(3, 1, 0, H)

@@ -109,20 +109,6 @@ def tile_picked_neuron_lin_relu_srt_e_kernel(tc, w, xT, b, offs, out):
         def gather(h, j, window):
             nc.vector.tensor_copy(grouped[h][:, :, j], window.indirect(lists[:, h * H // 16 : (h + 1) * H // 16]))
 
-        scrap = psum.tile([32, P], F32, name="scrap", tag="bank")
-
-        def exercise(count):
-            for i in range(count):
-                nc.tensor.matmul_mx(
-                    out=scrap[:],
-                    lhsT=codes[0][:, 0:32].bitcast(FP8X4),
-                    lhsT_scale=scales[0][:, 0:32],
-                    rhs=codes[0][:, 0:P].bitcast(FP8X4),
-                    rhs_scale=scales[0][:, 0:P],
-                    start=True,
-                    stop=True,
-                )
-
         for j in range(2):
             nc.vector.tensor_copy(picked[:, j, :], planes[j][:].indirect(lists[:]))
         weave(nc.scalar.copy, 0, 0)
@@ -131,7 +117,6 @@ def tile_picked_neuron_lin_relu_srt_e_kernel(tc, w, xT, b, offs, out):
             gather(h, 2, planes[2][:])
         gather(0, 3, planes[3][:, 0:FIRST])
         quantise_w(0, 0, H)
-        exercise(9)
         weave_x(nc.scalar.copy, 0, 0, 160)
         weave_x(nc.vector.tensor_copy, 0, 160, H)
         gather(1, 3, planes[3][:])

@@ -65,7 +65,10 @@ def tile_picked_neuron_lin_relu_srt_e_kernel(tc, w, xT, b, offs, out):
             copy(out=grouped[h][:, :, j0 : j0 + 2], in_=picked[:, j0 : j0 + 2, cols].rearrange("p j n -> p n j"))
 
         def weave_x(copy, h, lo, hi):
-            copy(out=x_grouped[h][:, lo:hi, :], in_=x_raw[h][:, :, lo:hi].rearrange("p j n -> p n j"))
+            copy(
+                out=x_grouped[h][:, lo:hi, :].rearrange("p (c i) j -> p c j i", i=4),
+                in_=x_raw[h][:, :, lo:hi].rearrange("p j (c i) -> p c j i", i=4),
+            )
 
         def quantise(codes_t, scales_t, grouped_t):
             nc.vector.quantize_mx(
@@ -117,8 +120,8 @@ def tile_picked_neuron_lin_relu_srt_e_kernel(tc, w, xT, b, offs, out):
             gather(h, 2, planes[2][:])
         gather(0, 3, planes[3][:, 0:FIRST])
         quantise_w(0, 0, H)
-        weave_x(nc.scalar.copy, 0, 0, 160)
-        weave_x(nc.vector.tensor_copy, 0, 160, H)
+        weave_x(nc.scalar.copy, 0, 0, P)
+        weave_x(nc.vector.tensor_copy, 0, P, H)
         gather(1, 3, planes[3][:])
         quantise_x(0, 0, P)
         quantise_x(0, P, H)

@@ -81,31 +81,32 @@ def tile_picked_neuron_lin_relu_srt_e_kernel(tc, w, xT, b, offs, out):
         def quantise_w(h, lo, hi):
             quantise(codes[h][:, lo:hi], scales[h][:, lo:hi], grouped[h][:, lo:hi, :])
 
-        def multiply(q, h, lo, hi):
+        def multiply(q, h, lo, hi, step):
             acc = psum.tile([P, hi - lo], F32, name="acc", tag="bank")
             cols = slice((q % 2) * P, (q % 2 + 1) * P)
-            nc.tensor.matmul_mx(
-                out=acc[:],
-                lhsT=codes[q // 2][:, cols].bitcast(FP8X4),
-                lhsT_scale=scales[q // 2][:, cols],
-                rhs=x_codes[h][:, lo:hi].bitcast(FP8X4),
-                rhs_scale=x_scales[h][:, lo:hi],
-                start=True,
-                stop=True,
-            )
+            for t in range(lo, hi, step):
+                nc.tensor.matmul_mx(
+                    out=acc[:, t - lo : t - lo + step],
+                    lhsT=codes[q // 2][:, cols].bitcast(FP8X4),
+                    lhsT_scale=scales[q // 2][:, cols],
+                    rhs=x_codes[h][:, t : t + step].bitcast(FP8X4),
+                    rhs_scale=x_scales[h][:, t : t + step],
+                    start=True,
+                    stop=True,
+                )
             return acc
 
         results = [[keep.tile([P, H], F32, name="result%d_%d" % (q, h)) for h in range(2)] for q in range(4)]
 
         def finish_scalar(q, h, lo, hi):
             result = results[q][h][:, lo:hi]
-            nc.scalar.activation(result, multiply(q, h, lo, hi)[:], RELU, bias=bias[:, 32 * q : 32 * q + 1])
+            nc.scalar.activation(result, multiply(q, h, lo, hi, P if h else hi - lo)[:], RELU, bias=bias[:, 32 * q : 32 * q + 1])
             nc.sync.dma_start(out[q * P : (q + 1) * P, h * H + lo : h * H + hi], result)
 
         def finish_vector(q, h, lo, hi):
             result = results[q][h][:, lo:hi]
             nc.vector.tensor_scalar(
-                result, multiply(q, h, lo, hi)[:], bias[:, 32 * q : 32 * q + 1], 0.0, op0=ADD, op1=MAX
+                result, multiply(q, h, lo, hi, P if h else hi - lo)[:], bias[:, 32 * q : 32 * q + 1], 0.0, op0=ADD, op1=MAX
             )
             nc.sync.dma_start(out[q * P : (q + 1) * P, h * H + lo : h * H + hi], result)
 
@@ -120,8 +121,8 @@ def tile_picked_neuron_lin_relu_srt_e_kernel(tc, w, xT, b, offs, out):
             gather(h, 2, planes[2][:])
         gather(0, 3, planes[3][:, 0:FIRST])
         quantise_w(0, 0, H)
-        weave_x(nc.scalar.copy, 0, 0, P)
-        weave_x(nc.vector.tensor_copy, 0, P, H)
+        weave_x(nc.scalar.copy, 0, 0, 176)
+        weave_x(nc.vector.tensor_copy, 0, 176, H)
         gather(1, 3, planes[3][:])
         quantise_x(0, 0, P)
         quantise_x(0, P, H)

@@ -17,7 +17,9 @@ RELU = mybir.ActivationFunctionType.Relu
 P = 128
 PACK = 4
 H = 256
+C = 128
 FIRST = N - H
+RESULT_SLOTS = {(1, 2): "woven1"}
 
 
 def tile_picked_neuron_lin_relu_srt_e_kernel(tc, w, xT, b, offs, out):
@@ -28,13 +30,17 @@ def tile_picked_neuron_lin_relu_srt_e_kernel(tc, w, xT, b, offs, out):
 
         w_rows = w.rearrange("(p j) n -> p j n", j=PACK)
         x_rows = xT.rearrange("(p j) t -> p j t", j=PACK)
+        out_rows = out.rearrange("(q p) t -> p q t", p=P)
 
         lists = keep.tile([P, S // 16], U16, name="lists")
         planes = [keep.tile([P, N], F32, name="plane%d" % j) for j in range(PACK)]
-        x_raw = [keep.tile([P, PACK, H], F32, name="x_raw%d" % h, tag="x_raw%d" % h, align_bytes=64) for h in range(2)]
+        x_raw = [keep.tile([P, PACK, C], F32, name="x_raw%d" % c, tag="x_raw%d" % c, align_bytes=64) for c in range(4)]
         b_rows = keep.tile([P, P], F32, name="b_rows", align_bytes=64)
         bias = keep.tile([P, P], F32, name="bias", align_bytes=64)
         warm = keep.tile([P, 1], F32, name="warm")
+
+        def load_x(c):
+            nc.sync.dma_start(x_raw[c][:], x_rows[:, :, c * C : (c + 1) * C])
 
         nc.vector.memset(b_rows[:], 0.0)
         nc.vector.memset(warm[:], 0.0)
@@ -47,27 +53,32 @@ def tile_picked_neuron_lin_relu_srt_e_kernel(tc, w, xT, b, offs, out):
         nc.sync.dma_start(planes[1][:], w_rows[:, 1, :])
         nc.sync.dma_start(planes[2][:], w_rows[:, 2, :])
         nc.sync.dma_start(planes[3][:, 0:FIRST], w_rows[:, 3, 0:FIRST])
-        nc.sync.dma_start(x_raw[0][:], x_rows[:, :, 0:H])
+        load_x(0)
         nc.sync.dma_start(planes[3][:, FIRST:N], w_rows[:, 3, FIRST:N])
-        nc.sync.dma_start(x_raw[1][:], x_rows[:, :, H:T])
+        load_x(1)
+        load_x(2)
+        load_x(3)
         nc.vector.transpose(bias[:], b_rows[:])
 
         picked = keep.tile([P, 2, S], F32, name="picked")
         grouped = [keep.tile([P, H, PACK], BF16, name="grouped%d" % h, align_bytes=64) for h in range(2)]
-        codes = [keep.tile([P, H], U32, name="codes0", align_bytes=64)]
-        scales = [keep.tile([P, H], U8, name="scales%d" % h, align_bytes=64) for h in range(2)]
-        x_grouped = [keep.tile([P, H, PACK], BF16, name="x_grouped%d" % h, tag="x_grouped%d" % h, align_bytes=64) for h in range(2)]
-        x_codes = [keep.tile([P, H], U32, name="x_codes%d" % h, align_bytes=64) for h in range(2)]
-        x_scales = [keep.tile([P, H], U8, name="x_scales%d" % h, align_bytes=64) for h in range(2)]
+        codes = {}
+        scales = [keep.tile([P, P], U8, name="scales%d" % q, align_bytes=64) for q in range(4)]
+        x_codes = [keep.tile([P, C], U32, name="x_codes%d" % c, align_bytes=64) for c in range(4)]
+        x_scales = [keep.tile([P, C], U8, name="x_scales%d" % c, align_bytes=64) for c in range(4)]
+        x_grouped = {}
+        results = {}
 
         def weave(copy, h, j0):
             cols = slice(h * H, (h + 1) * H)
             copy(out=grouped[h][:, :, j0 : j0 + 2], in_=picked[:, j0 : j0 + 2, cols].rearrange("p j n -> p n j"))
 
-        def weave_x(copy, h, lo, hi):
+        def weave_x(copy, c):
+            tile = keep.tile([P, C, PACK], BF16, name="x_grouped%d" % c, tag="woven%d" % (c % 2), align_bytes=64)
+            x_grouped.setdefault(c, tile)
             copy(
-                out=x_grouped[h][:, lo:hi, :].rearrange("p (c i) j -> p c j i", i=4),
-                in_=x_raw[h][:, :, lo:hi].rearrange("p j (c i) -> p c j i", i=4),
+                out=tile[:].rearrange("p (c i) j -> p c j i", i=4),
+                in_=x_raw[c][:].rearrange("p j (c i) -> p c j i", i=4),
             )
 
         def quantise(codes_t, scales_t, grouped_t):
@@ -75,40 +86,48 @@ def tile_picked_neuron_lin_relu_srt_e_kernel(tc, w, xT, b, offs, out):
                 out=codes_t.bitcast(FP8X4), scales=scales_t, in_=grouped_t.rearrange("p n j -> p (n j)")
             )
 
-        def quantise_x(h, lo, hi):
-            quantise(x_codes[h][:, lo:hi], x_scales[h][:, lo:hi], x_grouped[h][:, lo:hi, :])
+        def quantise_x(c):
+            quantise(x_codes[c][:], x_scales[c][:], x_grouped[c][:])
 
-        def quantise_w(h, lo, hi):
-            quantise(codes[h][:, lo:hi], scales[h][:, lo:hi], grouped[h][:, lo:hi, :])
+        def quantise_w(q):
+            if q == 0:
+                codes.setdefault(0, keep.tile([P, P], U32, name="codes_first", align_bytes=64)[:])
+            if q == 1:
+                rest = keep.tile([P, 3 * P], U32, name="codes_rest", tag="x_raw0", align_bytes=64)
+                for r in range(1, 4):
+                    codes.setdefault(r, rest[:, (r - 1) * P : r * P])
+            quantise(codes[q], scales[q][:], grouped[q // 2][:, (q % 2) * P : (q % 2 + 1) * P, :])
 
-        def multiply(q, h, lo, hi, step):
-            acc = psum.tile([P, hi - lo], F32, name="acc", tag="bank")
-            cols = slice((q % 2) * P, (q % 2 + 1) * P)
-            for t in range(lo, hi, step):
-                nc.tensor.matmul_mx(
-                    out=acc[:, t - lo : t - lo + step],
-                    lhsT=codes[q // 2][:, cols].bitcast(FP8X4),
-                    lhsT_scale=scales[q // 2][:, cols],
-                    rhs=x_codes[h][:, t : t + step].bitcast(FP8X4),
-                    rhs_scale=x_scales[h][:, t : t + step],
-                    start=True,
-                    stop=True,
-                )
+        def multiply(q, c):
+            acc = psum.tile([P, C], F32, name="acc", tag="bank")
+            nc.tensor.matmul_mx(
+                out=acc[:],
+                lhsT=codes[q].bitcast(FP8X4),
+                lhsT_scale=scales[q][:],
+                rhs=x_codes[c][:].bitcast(FP8X4),
+                rhs_scale=x_scales[c][:],
+                start=True,
+                stop=True,
+            )
             return acc
 
-        results = [[keep.tile([P, H], F32, name="result%d_%d" % (q, h)) for h in range(2)] for q in range(4)]
+        def result(q, c):
+            key = (q // 2, c)
+            if key not in results:
+                tag = RESULT_SLOTS.get(key, "result%d_%d" % key)
+                results.setdefault(key, keep.tile([P, 2, C], F32, name="result%d_%d" % key, tag=tag, align_bytes=64))
+            return results[key][:, q % 2, :]
 
-        def finish_scalar(q, h, lo, hi):
-            result = results[q][h][:, lo:hi]
-            nc.scalar.activation(result, multiply(q, h, lo, hi, P if h else hi - lo)[:], RELU, bias=bias[:, 32 * q : 32 * q + 1])
-            nc.sync.dma_start(out[q * P : (q + 1) * P, h * H + lo : h * H + hi], result)
+        def finish_scalar(q, c):
+            nc.scalar.activation(result(q, c), multiply(q, c)[:], RELU, bias=bias[:, 32 * q : 32 * q + 1])
 
-        def finish_vector(q, h, lo, hi):
-            result = results[q][h][:, lo:hi]
+        def finish_vector(q, c):
             nc.vector.tensor_scalar(
-                result, multiply(q, h, lo, hi, P if h else hi - lo)[:], bias[:, 32 * q : 32 * q + 1], 0.0, op0=ADD, op1=MAX
+                result(q, c), multiply(q, c)[:], bias[:, 32 * q : 32 * q + 1], 0.0, op0=ADD, op1=MAX
             )
-            nc.sync.dma_start(out[q * P : (q + 1) * P, h * H + lo : h * H + hi], result)
+
+        def store(h, c):
+            nc.sync.dma_start(out_rows[:, 2 * h : 2 * h + 2, c * C : (c + 1) * C], results[(h, c)][:])
 
         def gather(h, j, window):
             nc.vector.tensor_copy(grouped[h][:, :, j], window.indirect(lists[:, h * H // 16 : (h + 1) * H // 16]))
@@ -120,25 +139,40 @@ def tile_picked_neuron_lin_relu_srt_e_kernel(tc, w, xT, b, offs, out):
         for h in range(2):
             gather(h, 2, planes[2][:])
         gather(0, 3, planes[3][:, 0:FIRST])
-        quantise_w(0, 0, H)
-        weave_x(nc.scalar.copy, 0, 0, 176)
-        weave_x(nc.vector.tensor_copy, 0, 176, H)
+        weave_x(nc.scalar.copy, 0)
         gather(1, 3, planes[3][:])
-        quantise_x(0, 0, P)
-        quantise_x(0, P, H)
-        codes.append(keep.tile([P, H], U32, name="codes1", tag="x_raw0", align_bytes=64))
-        quantise_w(1, 0, P)
-        quantise_w(1, P, H)
-        weave_x(nc.vector.tensor_copy, 1, 0, P)
-        weave_x(nc.vector.tensor_copy, 1, P, H)
-        quantise_x(1, 0, P)
-        quantise_x(1, P, H)
-        finish_scalar(0, 0, 0, P)
-        finish_scalar(0, 0, P, H)
-        for q in range(1, 4):
-            finish_scalar(q, 0, 0, H)
-        finish_scalar(0, 1, 0, P)
-        finish_vector(0, 1, P, H)
-        finish_scalar(1, 1, 0, H)
-        finish_vector(2, 1, 0, H)
-        finish_scalar(3, 1, 0, H)
+        weave_x(nc.scalar.copy, 1)
+        quantise_w(0)
+        quantise_x(0)
+        quantise_w(1)
+        quantise_w(2)
+        quantise_w(3)
+        quantise_x(1)
+        weave_x(nc.vector.tensor_copy, 2)
+        weave_x(nc.vector.tensor_copy, 3)
+        quantise_x(2)
+        quantise_x(3)
+        finish_scalar(0, 0)
+        finish_scalar(1, 0)
+        store(0, 0)
+        finish_scalar(2, 0)
+        finish_scalar(3, 0)
+        store(1, 0)
+        finish_scalar(0, 1)
+        finish_scalar(1, 1)
+        store(0, 1)
+        finish_scalar(2, 1)
+        finish_scalar(3, 1)
+        store(1, 1)
+        finish_scalar(0, 2)
+        finish_vector(2, 2)
+        finish_scalar(1, 2)
+        store(0, 2)
+        finish_vector(3, 2)
+        store(1, 2)
+        finish_scalar(0, 3)
+        finish_vector(1, 3)
+        store(0, 3)
+        finish_scalar(2, 3)
+        finish_vector(3, 3)
+        store(1, 3)

@@ -32,19 +32,16 @@ def tile_picked_neuron_lin_relu_srt_e_kernel(tc, w, xT, b, offs, out):
         x_rows = xT.rearrange("(p j) t -> p j t", j=PACK)
         out_rows = out.rearrange("(q p) t -> p q t", p=P)
 
-        lists = keep.tile([P, S // 16], U16, name="lists")
-        planes = [keep.tile([P, N], F32, name="plane%d" % j) for j in range(PACK)]
-        x_raw = [keep.tile([P, PACK, C], F32, name="x_raw%d" % c, tag="x_raw%d" % c, align_bytes=64) for c in range(4)]
-        b_rows = keep.tile([P, P], F32, name="b_rows", align_bytes=64)
-        bias = keep.tile([P, P], F32, name="bias", align_bytes=64)
-        warm = keep.tile([P, 1], F32, name="warm")
+        lists = keep.tile([P, S // 16], U16, name="lists", align_bytes=256)
+        planes = [keep.tile([P, N], F32, name="plane%d" % j, align_bytes=256) for j in range(PACK)]
+        x_raw = [keep.tile([P, PACK, C], F32, name="x_raw%d" % c, tag="x_raw%d" % c, align_bytes=256) for c in range(4)]
+        b_rows = keep.tile([P, P], F32, name="b_rows", align_bytes=256)
+        bias = keep.tile([P, P], F32, name="bias", align_bytes=256)
 
         def load_x(c):
             nc.sync.dma_start(x_raw[c][:], x_rows[:, :, c * C : (c + 1) * C])
 
         nc.vector.memset(b_rows[:], 0.0)
-        nc.vector.memset(warm[:], 0.0)
-        nc.scalar.activation(warm[:], warm[:], RELU)
         nc.sync.dma_start(planes[0][:], w_rows[:, 0, :])
         nc.sync.dma_start(lists[:], offs)
         nc.sync.dma_start(
@@ -60,12 +57,12 @@ def tile_picked_neuron_lin_relu_srt_e_kernel(tc, w, xT, b, offs, out):
         load_x(3)
         nc.vector.transpose(bias[:], b_rows[:])
 
-        picked = keep.tile([P, 2, S], F32, name="picked")
-        grouped = [keep.tile([P, H, PACK], BF16, name="grouped%d" % h, align_bytes=64) for h in range(2)]
+        picked = keep.tile([P, 2, S], F32, name="picked", align_bytes=256)
+        grouped = [keep.tile([P, H, PACK], BF16, name="grouped%d" % h, align_bytes=256) for h in range(2)]
         codes = {}
-        scales = [keep.tile([P, P], U8, name="scales%d" % q, align_bytes=64) for q in range(4)]
-        x_codes = [keep.tile([P, C], U32, name="x_codes%d" % c, align_bytes=64) for c in range(4)]
-        x_scales = [keep.tile([P, C], U8, name="x_scales%d" % c, align_bytes=64) for c in range(4)]
+        scales = [keep.tile([P, P], U8, name="scales%d" % q, align_bytes=256) for q in range(4)]
+        x_codes = [keep.tile([P, C], U32, name="x_codes%d" % c, align_bytes=256) for c in range(4)]
+        x_scales = [keep.tile([P, C], U8, name="x_scales%d" % c, align_bytes=256) for c in range(4)]
         x_grouped = {}
         results = {}
 
@@ -74,7 +71,7 @@ def tile_picked_neuron_lin_relu_srt_e_kernel(tc, w, xT, b, offs, out):
             copy(out=grouped[h][:, :, j0 : j0 + 2], in_=picked[:, j0 : j0 + 2, cols].rearrange("p j n -> p n j"))
 
         def weave_x(copy, c):
-            tile = keep.tile([P, C, PACK], BF16, name="x_grouped%d" % c, tag="woven%d" % (c % 2), align_bytes=64)
+            tile = keep.tile([P, C, PACK], BF16, name="x_grouped%d" % c, tag="woven%d" % (c % 2), align_bytes=256)
             x_grouped.setdefault(c, tile)
             copy(
                 out=tile[:].rearrange("p (c i) j -> p c j i", i=4),
@@ -91,9 +88,9 @@ def tile_picked_neuron_lin_relu_srt_e_kernel(tc, w, xT, b, offs, out):
 
         def quantise_w(q):
             if q == 0:
-                codes.setdefault(0, keep.tile([P, P], U32, name="codes_first", align_bytes=64)[:])
+                codes.setdefault(0, keep.tile([P, P], U32, name="codes_first", align_bytes=256)[:])
             if q == 1:
-                rest = keep.tile([P, 3 * P], U32, name="codes_rest", tag="x_raw0", align_bytes=64)
+                rest = keep.tile([P, 3 * P], U32, name="codes_rest", tag="x_raw0", align_bytes=256)
                 for r in range(1, 4):
                     codes.setdefault(r, rest[:, (r - 1) * P : r * P])
             quantise(codes[q], scales[q][:], grouped[q // 2][:, (q % 2) * P : (q % 2 + 1) * P, :])
@@ -115,7 +112,7 @@ def tile_picked_neuron_lin_relu_srt_e_kernel(tc, w, xT, b, offs, out):
             key = (q // 2, c)
             if key not in results:
                 tag = RESULT_SLOTS.get(key, "result%d_%d" % key)
-                results.setdefault(key, keep.tile([P, 2, C], F32, name="result%d_%d" % key, tag=tag, align_bytes=64))
+                results.setdefault(key, keep.tile([P, 2, C], F32, name="result%d_%d" % key, tag=tag, align_bytes=256))
             return results[key][:, q % 2, :]
 
         def finish_scalar(q, c):

@@ -1,6 +1,7 @@
 from contextlib import ExitStack
 
 import concourse.mybir as mybir
+from concourse.masks import make_identity
 
 K, N, T, S = 512, 2048, 512, 512
 FLOPS = 2 * K * S * T
@@ -35,27 +36,29 @@ def tile_picked_neuron_lin_relu_srt_e_kernel(tc, w, xT, b, offs, out):
         lists = keep.tile([P, S // 16], U16, name="lists", align_bytes=256)
         planes = [keep.tile([P, N], F32, name="plane%d" % j, align_bytes=256) for j in range(PACK)]
         x_raw = [keep.tile([P, PACK, C], F32, name="x_raw%d" % c, tag="x_raw%d" % c, align_bytes=256) for c in range(4)]
-        b_rows = keep.tile([P, P], F32, name="b_rows", align_bytes=256)
-        bias = keep.tile([P, P], F32, name="bias", align_bytes=256)
+        b_rows = keep.tile([P, P], F32, name="b_rows", tag="b_rows", align_bytes=256)
+        bias = keep.tile([P, 4], F32, name="bias", align_bytes=256)
+        identity = keep.tile([P, P], F32, name="identity", align_bytes=256)
 
         def load_x(c):
             nc.sync.dma_start(x_raw[c][:], x_rows[:, :, c * C : (c + 1) * C])
 
         nc.vector.memset(b_rows[:], 0.0)
+        make_identity(nc, identity[:])
         nc.sync.dma_start(planes[0][:], w_rows[:, 0, :])
         nc.sync.dma_start(lists[:], offs)
-        nc.sync.dma_start(
-            b_rows[0:P:32, :].rearrange("r (q i) -> r q i", i=32), b.rearrange("(q r i) o -> r q (i o)", r=4, i=32)
-        )
         nc.sync.dma_start(planes[1][:], w_rows[:, 1, :])
         nc.sync.dma_start(planes[2][:], w_rows[:, 2, :])
         nc.sync.dma_start(planes[3][:, 0:FIRST], w_rows[:, 3, 0:FIRST])
-        load_x(0)
         nc.sync.dma_start(planes[3][:, FIRST:N], w_rows[:, 3, FIRST:N])
+        nc.sync.dma_start(b_rows[0:4, :], b.rearrange("(q i) o -> q (i o)", q=4))
+        load_x(0)
         load_x(1)
         load_x(2)
         load_x(3)
-        nc.vector.transpose(bias[:], b_rows[:])
+        turned = psum.tile([P, P], F32, name="turned", tag="bank")
+        nc.tensor.transpose(turned[:], b_rows[:], identity[:])
+        nc.scalar.copy(out=bias[:], in_=turned[:, 0:4])
 
         picked = keep.tile([P, 2, S], F32, name="picked", align_bytes=256)
         grouped = [keep.tile([P, H, PACK], BF16, name="grouped%d" % h, align_bytes=256) for h in range(2)]
@@ -88,11 +91,13 @@ def tile_picked_neuron_lin_relu_srt_e_kernel(tc, w, xT, b, offs, out):
 
         def quantise_w(q):
             if q == 0:
-                codes.setdefault(0, keep.tile([P, P], U32, name="codes_first", align_bytes=256)[:])
-            if q == 1:
-                rest = keep.tile([P, 3 * P], U32, name="codes_rest", tag="x_raw0", align_bytes=256)
-                for r in range(1, 4):
-                    codes.setdefault(r, rest[:, (r - 1) * P : r * P])
+                first = keep.tile([P, 2 * P], U32, name="codes_first", tag="b_rows", align_bytes=256)
+                for r in range(2):
+                    codes.setdefault(r, first[:, r * P : (r + 1) * P])
+            if q == 2:
+                rest = keep.tile([P, 2 * P], U32, name="codes_rest", tag="x_raw0", align_bytes=256)
+                for r in range(2, 4):
+                    codes.setdefault(r, rest[:, (r - 2) * P : (r - 1) * P])
             quantise(codes[q], scales[q][:], grouped[q // 2][:, (q % 2) * P : (q % 2 + 1) * P, :])
 
         def multiply(q, c):
@@ -116,11 +121,11 @@ def tile_picked_neuron_lin_relu_srt_e_kernel(tc, w, xT, b, offs, out):
             return results[key][:, q % 2, :]
 
         def finish_scalar(q, c):
-            nc.scalar.activation(result(q, c), multiply(q, c)[:], RELU, bias=bias[:, 32 * q : 32 * q + 1])
+            nc.scalar.activation(result(q, c), multiply(q, c)[:], RELU, bias=bias[:, q : q + 1])
 
         def finish_vector(q, c):
             nc.vector.tensor_scalar(
-                result(q, c), multiply(q, c)[:], bias[:, 32 * q : 32 * q + 1], 0.0, op0=ADD, op1=MAX
+                result(q, c), multiply(q, c)[:], bias[:, q : q + 1], 0.0, op0=ADD, op1=MAX
             )
 
         def store(h, c):
@@ -140,8 +145,8 @@ def tile_picked_neuron_lin_relu_srt_e_kernel(tc, w, xT, b, offs, out):
         gather(1, 3, planes[3][:])
         weave_x(nc.scalar.copy, 1)
         quantise_w(0)
-        quantise_x(0)
         quantise_w(1)
+        quantise_x(0)
         quantise_w(2)
         quantise_w(3)
         quantise_x(1)

@@ -45,26 +45,27 @@ def tile_picked_neuron_lin_relu_srt_e_kernel(tc, w, xT, b, offs, out):
 
         nc.vector.memset(b_rows[:], 0.0)
         make_identity(nc, identity[:])
-        nc.sync.dma_start(planes[0][:], w_rows[:, 0, :])
-        nc.sync.dma_start(lists[:], offs)
-        nc.sync.dma_start(planes[1][:], w_rows[:, 1, :])
         nc.sync.dma_start(planes[2][:], w_rows[:, 2, :])
+        nc.sync.dma_start(lists[:], offs)
+        nc.sync.dma_start(planes[0][:], w_rows[:, 0, :])
+        nc.sync.dma_start(planes[1][:], w_rows[:, 1, :])
         nc.sync.dma_start(planes[3][:, 0:FIRST], w_rows[:, 3, 0:FIRST])
         nc.sync.dma_start(planes[3][:, FIRST:N], w_rows[:, 3, FIRST:N])
-        nc.sync.dma_start(b_rows[0:4, :], b.rearrange("(q i) o -> q (i o)", q=4))
         load_x(0)
+        nc.sync.dma_start(b_rows[0:4, :], b.rearrange("(q i) o -> q (i o)", q=4))
         load_x(1)
         load_x(2)
         load_x(3)
         turned = psum.tile([P, P], F32, name="turned", tag="bank")
         nc.tensor.transpose(turned[:], b_rows[:], identity[:])
-        nc.scalar.copy(out=bias[:], in_=turned[:, 0:4])
 
         picked = keep.tile([P, 2, S], F32, name="picked", align_bytes=256)
         grouped = [keep.tile([P, H, PACK], BF16, name="grouped%d" % h, align_bytes=256) for h in range(2)]
-        codes = {}
+        held = keep.tile([P, 4 * P + C], U32, name="held", tag="b_rows", align_bytes=256)
+        codes = [held[:, q * P : (q + 1) * P] for q in range(4)]
         scales = [keep.tile([P, P], U8, name="scales%d" % q, align_bytes=256) for q in range(4)]
-        x_codes = [keep.tile([P, C], U32, name="x_codes%d" % c, align_bytes=256) for c in range(4)]
+        x_codes = [held[:, 4 * P :]]
+        x_codes.extend(keep.tile([P, C], U32, name="x_codes%d" % c, align_bytes=256)[:] for c in range(1, 4))
         x_scales = [keep.tile([P, C], U8, name="x_scales%d" % c, align_bytes=256) for c in range(4)]
         x_grouped = {}
         results = {}
@@ -87,17 +88,9 @@ def tile_picked_neuron_lin_relu_srt_e_kernel(tc, w, xT, b, offs, out):
             )
 
         def quantise_x(c):
-            quantise(x_codes[c][:], x_scales[c][:], x_grouped[c][:])
+            quantise(x_codes[c], x_scales[c][:], x_grouped[c][:])
 
         def quantise_w(q):
-            if q == 0:
-                first = keep.tile([P, 2 * P], U32, name="codes_first", tag="b_rows", align_bytes=256)
-                for r in range(2):
-                    codes.setdefault(r, first[:, r * P : (r + 1) * P])
-            if q == 2:
-                rest = keep.tile([P, 2 * P], U32, name="codes_rest", tag="x_raw0", align_bytes=256)
-                for r in range(2, 4):
-                    codes.setdefault(r, rest[:, (r - 2) * P : (r - 1) * P])
             quantise(codes[q], scales[q][:], grouped[q // 2][:, (q % 2) * P : (q % 2 + 1) * P, :])
 
         def multiply(q, c):
@@ -106,7 +99,7 @@ def tile_picked_neuron_lin_relu_srt_e_kernel(tc, w, xT, b, offs, out):
                 out=acc[:],
                 lhsT=codes[q].bitcast(FP8X4),
                 lhsT_scale=scales[q][:],
-                rhs=x_codes[c][:].bitcast(FP8X4),
+                rhs=x_codes[c].bitcast(FP8X4),
                 rhs_scale=x_scales[c][:],
                 start=True,
                 stop=True,
@@ -134,19 +127,21 @@ def tile_picked_neuron_lin_relu_srt_e_kernel(tc, w, xT, b, offs, out):
         def gather(h, j, window):
             nc.vector.tensor_copy(grouped[h][:, :, j], window.indirect(lists[:, h * H // 16 : (h + 1) * H // 16]))
 
-        for j in range(2):
-            nc.vector.tensor_copy(picked[:, j, :], planes[j][:].indirect(lists[:]))
-        weave(nc.scalar.copy, 0, 0)
-        weave(nc.scalar.copy, 1, 0)
         for h in range(2):
             gather(h, 2, planes[2][:])
+        nc.vector.tensor_copy(picked[:, 0, :], planes[0][:].indirect(lists[:]))
+        for h in range(2):
+            entries = lists[:, h * H // 16 : (h + 1) * H // 16]
+            nc.vector.tensor_copy(picked[:, 1, h * H : (h + 1) * H], planes[1][:].indirect(entries))
+            weave(nc.scalar.copy, h, 0)
         gather(0, 3, planes[3][:, 0:FIRST])
         weave_x(nc.scalar.copy, 0)
+        nc.scalar.copy(out=bias[:], in_=turned[:, 0:4])
         gather(1, 3, planes[3][:])
         weave_x(nc.scalar.copy, 1)
         quantise_w(0)
-        quantise_w(1)
         quantise_x(0)
+        quantise_w(1)
         quantise_w(2)
         quantise_w(3)
         quantise_x(1)

@@ -55,7 +55,8 @@ def tile_picked_neuron_lin_relu_srt_e_kernel(tc, w, xT, b, offs, out):
         nc.sync.dma_start(b_rows[0:4, :], b.rearrange("(q i) o -> q (i o)", q=4))
         load_x(1)
         load_x(2)
-        load_x(3)
+        for j in range(PACK):
+            nc.sync.dma_start(x_raw[3][:, j, :], x_rows[:, j, 3 * C : 4 * C])
         turned = psum.tile([P, P], F32, name="turned", tag="bank")
         nc.tensor.transpose(turned[:], b_rows[:], identity[:])
 
@@ -106,6 +107,9 @@ def tile_picked_neuron_lin_relu_srt_e_kernel(tc, w, xT, b, offs, out):
             )
             return acc
 
+        def store_block(q, c):
+            nc.sync.dma_start(out_rows[:, q, c * C : (c + 1) * C], results[(q // 2, c)][:, q % 2, :])
+
         def result(q, c):
             key = (q // 2, c)
             if key not in results:
@@ -150,8 +154,9 @@ def tile_picked_neuron_lin_relu_srt_e_kernel(tc, w, xT, b, offs, out):
         quantise_x(2)
         quantise_x(3)
         finish_scalar(0, 0)
+        store_block(0, 0)
         finish_scalar(1, 0)
-        store(0, 0)
+        store_block(1, 0)
         finish_scalar(2, 0)
         finish_scalar(3, 0)
         store(1, 0)

@@ -34,7 +34,9 @@ def tile_picked_neuron_lin_relu_srt_e_kernel(tc, w, xT, b, offs, out):
         out_rows = out.rearrange("(q p) t -> p q t", p=P)
 
         lists = keep.tile([P, S // 16], U16, name="lists", align_bytes=256)
-        planes = [keep.tile([P, N], F32, name="plane%d" % j, align_bytes=256) for j in range(PACK)]
+        early = keep.tile([P, 2, N], F32, name="early", align_bytes=256)
+        planes = [early[:, 0, :], early[:, 1, :]]
+        planes.extend(keep.tile([P, N], F32, name="plane%d" % j, align_bytes=256)[:] for j in range(2, PACK))
         x_raw = [keep.tile([P, PACK, C], F32, name="x_raw%d" % c, tag="x_raw%d" % c, align_bytes=256) for c in range(4)]
         b_rows = keep.tile([P, P], F32, name="b_rows", tag="b_rows", align_bytes=256)
         bias = keep.tile([P, 4], F32, name="bias", align_bytes=256)
@@ -45,16 +47,16 @@ def tile_picked_neuron_lin_relu_srt_e_kernel(tc, w, xT, b, offs, out):
 
         nc.vector.memset(b_rows[:], 0.0)
         make_identity(nc, identity[:])
-        nc.sync.dma_start(planes[2][:], w_rows[:, 2, :])
+        nc.sync.dma_start(early[:], w_rows[:, 0:2, :])
         nc.sync.dma_start(lists[:], offs)
-        nc.sync.dma_start(planes[0][:], w_rows[:, 0, :])
-        nc.sync.dma_start(planes[1][:], w_rows[:, 1, :])
+        nc.sync.dma_start(planes[2], w_rows[:, 2, :])
         nc.sync.dma_start(planes[3][:, 0:FIRST], w_rows[:, 3, 0:FIRST])
         nc.sync.dma_start(planes[3][:, FIRST:N], w_rows[:, 3, FIRST:N])
         load_x(0)
         nc.sync.dma_start(b_rows[0:4, :], b.rearrange("(q i) o -> q (i o)", q=4))
         load_x(1)
-        load_x(2)
+        for j in range(0, PACK, 2):
+            nc.sync.dma_start(x_raw[2][:, j : j + 2, :], x_rows[:, j : j + 2, 2 * C : 3 * C])
         for j in range(PACK):
             nc.sync.dma_start(x_raw[3][:, j, :], x_rows[:, j, 3 * C : 4 * C])
         turned = psum.tile([P, P], F32, name="turned", tag="bank")
@@ -131,17 +133,15 @@ def tile_picked_neuron_lin_relu_srt_e_kernel(tc, w, xT, b, offs, out):
         def gather(h, j, window):
             nc.vector.tensor_copy(grouped[h][:, :, j], window.indirect(lists[:, h * H // 16 : (h + 1) * H // 16]))
 
+        for j in range(2):
+            nc.vector.tensor_copy(picked[:, j, :], planes[j].indirect(lists[:]))
         for h in range(2):
-            gather(h, 2, planes[2][:])
-        nc.vector.tensor_copy(picked[:, 0, :], planes[0][:].indirect(lists[:]))
-        for h in range(2):
-            entries = lists[:, h * H // 16 : (h + 1) * H // 16]
-            nc.vector.tensor_copy(picked[:, 1, h * H : (h + 1) * H], planes[1][:].indirect(entries))
             weave(nc.scalar.copy, h, 0)
+            gather(h, 2, planes[2])
         gather(0, 3, planes[3][:, 0:FIRST])
         weave_x(nc.scalar.copy, 0)
         nc.scalar.copy(out=bias[:], in_=turned[:, 0:4])
-        gather(1, 3, planes[3][:])
+        gather(1, 3, planes[3])
         weave_x(nc.scalar.copy, 1)
         quantise_w(0)
         quantise_x(0)

@@ -33,14 +33,14 @@ def tile_picked_neuron_lin_relu_srt_e_kernel(tc, w, xT, b, offs, out):
         x_rows = xT.rearrange("(p j) t -> p j t", j=PACK)
         out_rows = out.rearrange("(q p) t -> p q t", p=P)
 
-        lists = keep.tile([P, S // 16], U16, name="lists", align_bytes=256)
-        early = keep.tile([P, 2, N], F32, name="early", align_bytes=256)
+        lists = keep.tile([P, S // 16], U16, name="lists", align_bytes=512)
+        early = keep.tile([P, 2, N], F32, name="early", align_bytes=512)
         planes = [early[:, 0, :], early[:, 1, :]]
-        planes.extend(keep.tile([P, N], F32, name="plane%d" % j, align_bytes=256)[:] for j in range(2, PACK))
-        x_raw = [keep.tile([P, PACK, C], F32, name="x_raw%d" % c, tag="x_raw%d" % c, align_bytes=256) for c in range(4)]
-        b_rows = keep.tile([P, P], F32, name="b_rows", tag="b_rows", align_bytes=256)
-        bias = keep.tile([P, 4], F32, name="bias", align_bytes=256)
-        identity = keep.tile([P, P], F32, name="identity", align_bytes=256)
+        planes.extend(keep.tile([P, N], F32, name="plane%d" % j, align_bytes=512)[:] for j in range(2, PACK))
+        x_raw = [keep.tile([P, PACK, C], F32, name="x_raw%d" % c, tag="x_raw%d" % c, align_bytes=512) for c in range(4)]
+        b_rows = keep.tile([P, P], F32, name="b_rows", tag="b_rows", align_bytes=512)
+        bias = keep.tile([P, 4], F32, name="bias", align_bytes=512)
+        identity = keep.tile([P, P], F32, name="identity", align_bytes=512)
 
         def load_x(c):
             nc.sync.dma_start(x_raw[c][:], x_rows[:, :, c * C : (c + 1) * C])
@@ -62,14 +62,14 @@ def tile_picked_neuron_lin_relu_srt_e_kernel(tc, w, xT, b, offs, out):
         turned = psum.tile([P, P], F32, name="turned", tag="bank")
         nc.tensor.transpose(turned[:], b_rows[:], identity[:])
 
-        picked = keep.tile([P, 2, S], F32, name="picked", align_bytes=256)
-        grouped = [keep.tile([P, H, PACK], BF16, name="grouped%d" % h, align_bytes=256) for h in range(2)]
-        held = keep.tile([P, 4 * P + C], U32, name="held", tag="b_rows", align_bytes=256)
+        picked = keep.tile([P, 2, S], F32, name="picked", align_bytes=512)
+        grouped = [keep.tile([P, H, PACK], BF16, name="grouped%d" % h, align_bytes=512) for h in range(2)]
+        held = keep.tile([P, 4 * P + C], U32, name="held", tag="b_rows", align_bytes=512)
         codes = [held[:, q * P : (q + 1) * P] for q in range(4)]
-        scales = [keep.tile([P, P], U8, name="scales%d" % q, align_bytes=256) for q in range(4)]
+        scales = [keep.tile([P, P], U8, name="scales%d" % q, align_bytes=512) for q in range(4)]
         x_codes = [held[:, 4 * P :]]
-        x_codes.extend(keep.tile([P, C], U32, name="x_codes%d" % c, align_bytes=256)[:] for c in range(1, 4))
-        x_scales = [keep.tile([P, C], U8, name="x_scales%d" % c, align_bytes=256) for c in range(4)]
+        x_codes.extend(keep.tile([P, C], U32, name="x_codes%d" % c, align_bytes=512)[:] for c in range(1, 4))
+        x_scales = [keep.tile([P, C], U8, name="x_scales%d" % c, align_bytes=512) for c in range(4)]
         x_grouped = {}
         results = {}
 
@@ -78,7 +78,7 @@ def tile_picked_neuron_lin_relu_srt_e_kernel(tc, w, xT, b, offs, out):
             copy(out=grouped[h][:, :, j0 : j0 + 2], in_=picked[:, j0 : j0 + 2, cols].rearrange("p j n -> p n j"))
 
         def weave_x(copy, c):
-            tile = keep.tile([P, C, PACK], BF16, name="x_grouped%d" % c, tag="woven%d" % (c % 2), align_bytes=256)
+            tile = keep.tile([P, C, PACK], BF16, name="x_grouped%d" % c, tag="woven%d" % (c % 2), align_bytes=512)
             x_grouped.setdefault(c, tile)
             copy(
                 out=tile[:].rearrange("p (c i) j -> p c j i", i=4),
@@ -116,7 +116,7 @@ def tile_picked_neuron_lin_relu_srt_e_kernel(tc, w, xT, b, offs, out):
             key = (q // 2, c)
             if key not in results:
                 tag = RESULT_SLOTS.get(key, "result%d_%d" % key)
-                results.setdefault(key, keep.tile([P, 2, C], F32, name="result%d_%d" % key, tag=tag, align_bytes=256))
+                results.setdefault(key, keep.tile([P, 2, C], F32, name="result%d_%d" % key, tag=tag, align_bytes=512))
             return results[key][:, q % 2, :]
 
         def finish_scalar(q, c):

@@ -17,10 +17,11 @@ RELU = mybir.ActivationFunctionType.Relu
 
 P = 128
 PACK = 4
-H = 256
+BLOCKS = S // P
+H = S // 2
 C = 128
 FIRST = N - H
-RESULT_SLOTS = {(1, 2): "woven1"}
+ALIGN = 256
 
 
 def tile_picked_neuron_lin_relu_srt_e_kernel(tc, w, xT, b, offs, out):
@@ -29,152 +30,131 @@ def tile_picked_neuron_lin_relu_srt_e_kernel(tc, w, xT, b, offs, out):
         keep = ctx.enter_context(tc.tile_pool(name="keep", bufs=1))
         psum = ctx.enter_context(tc.psum_pool(name="psum", bufs=8))
 
+        def sbuf(name, shape, dtype, slot=None):
+            return keep.tile(shape, dtype, name=name, tag=slot or name, align_bytes=ALIGN)
+
         w_rows = w.rearrange("(p j) n -> p j n", j=PACK)
         x_rows = xT.rearrange("(p j) t -> p j t", j=PACK)
         out_rows = out.rearrange("(q p) t -> p q t", p=P)
 
-        lists = keep.tile([P, S // 16], U16, name="lists", align_bytes=512)
-        early = keep.tile([P, 2, N], F32, name="early", align_bytes=512)
-        planes = [early[:, 0, :], early[:, 1, :]]
-        planes.extend(keep.tile([P, N], F32, name="plane%d" % j, align_bytes=512)[:] for j in range(2, PACK))
-        x_raw = [keep.tile([P, PACK, C], F32, name="x_raw%d" % c, tag="x_raw%d" % c, align_bytes=512) for c in range(4)]
-        b_rows = keep.tile([P, P], F32, name="b_rows", tag="b_rows", align_bytes=512)
-        bias = keep.tile([P, 4], F32, name="bias", align_bytes=512)
-        identity = keep.tile([P, P], F32, name="identity", align_bytes=512)
+        x_cuts = (0, C, 2 * C, T - C // 2, T)
+        lists = sbuf("lists", [P, S // 16], U16)
+        planes01 = sbuf("planes01", [P, 2, N], F32)
+        plane2 = sbuf("plane2", [P, N], F32)
+        plane3 = sbuf("plane3", [P, N], F32)
+        x_raw = [sbuf("x_raw%d" % n, [P, PACK, x_cuts[n + 1] - x_cuts[n]], F32) for n in range(4)]
+        b_rows = sbuf("b_rows", [P, P], F32)
+        bias = sbuf("bias", [P, BLOCKS], F32)
+        identity = sbuf("identity", [P, P], F32)
 
-        def load_x(c):
-            nc.sync.dma_start(x_raw[c][:], x_rows[:, :, c * C : (c + 1) * C])
+        def load_x(n, planes_at_once):
+            for j in range(0, PACK, planes_at_once):
+                rows = slice(j, j + planes_at_once)
+                nc.sync.dma_start(x_raw[n][:, rows, :], x_rows[:, rows, x_cuts[n] : x_cuts[n + 1]])
 
         nc.vector.memset(b_rows[:], 0.0)
         make_identity(nc, identity[:])
-        nc.sync.dma_start(early[:], w_rows[:, 0:2, :])
+        nc.sync.dma_start(planes01[:], w_rows[:, 0:2, :])
         nc.sync.dma_start(lists[:], offs)
-        nc.sync.dma_start(planes[2], w_rows[:, 2, :])
-        nc.sync.dma_start(planes[3][:, 0:FIRST], w_rows[:, 3, 0:FIRST])
-        nc.sync.dma_start(planes[3][:, FIRST:N], w_rows[:, 3, FIRST:N])
-        load_x(0)
-        nc.sync.dma_start(b_rows[0:4, :], b.rearrange("(q i) o -> q (i o)", q=4))
-        load_x(1)
-        for j in range(0, PACK, 2):
-            nc.sync.dma_start(x_raw[2][:, j : j + 2, :], x_rows[:, j : j + 2, 2 * C : 3 * C])
-        for j in range(PACK):
-            nc.sync.dma_start(x_raw[3][:, j, :], x_rows[:, j, 3 * C : 4 * C])
+        nc.sync.dma_start(plane2[:], w_rows[:, 2, :])
+        nc.sync.dma_start(plane3[:, 0:FIRST], w_rows[:, 3, 0:FIRST])
+        nc.sync.dma_start(plane3[:, FIRST:N], w_rows[:, 3, FIRST:N])
+        load_x(0, PACK)
+        nc.sync.dma_start(b_rows[0:BLOCKS, :], b.rearrange("(q i) o -> q (i o)", q=BLOCKS))
+        load_x(1, PACK)
+        load_x(2, 2)
+        load_x(3, 2)
         turned = psum.tile([P, P], F32, name="turned", tag="bank")
         nc.tensor.transpose(turned[:], b_rows[:], identity[:])
 
-        picked = keep.tile([P, 2, S], F32, name="picked", align_bytes=512)
-        grouped = [keep.tile([P, H, PACK], BF16, name="grouped%d" % h, align_bytes=512) for h in range(2)]
-        held = keep.tile([P, 4 * P + C], U32, name="held", tag="b_rows", align_bytes=512)
-        codes = [held[:, q * P : (q + 1) * P] for q in range(4)]
-        scales = [keep.tile([P, P], U8, name="scales%d" % q, align_bytes=512) for q in range(4)]
-        x_codes = [held[:, 4 * P :]]
-        x_codes.extend(keep.tile([P, C], U32, name="x_codes%d" % c, align_bytes=512)[:] for c in range(1, 4))
-        x_scales = [keep.tile([P, C], U8, name="x_scales%d" % c, align_bytes=512) for c in range(4)]
-        x_grouped = {}
-        results = {}
+        picked = sbuf("picked", [P, 2, S], F32)
+        w_woven = [sbuf("w_woven%d" % h, [P, H, PACK], BF16) for h in range(2)]
+        held = sbuf("held", [P, S + C], U32, slot="b_rows")
+        w_codes = [held[:, q * P : (q + 1) * P] for q in range(BLOCKS)]
+        w_scales = [sbuf("w_scales%d" % q, [P, P], U8) for q in range(BLOCKS)]
+        x_codes = [held[:, S:]] + [sbuf("x_codes%d" % c, [P, C], U32)[:] for c in range(1, 4)]
+        x_scales = [sbuf("x_scales%d" % c, [P, C], U8) for c in range(4)]
 
-        def weave(copy, h, j0):
+        def gather(h, j, window):
+            nc.vector.tensor_copy(w_woven[h][:, :, j], window.indirect(lists[:, h * H // 16 : (h + 1) * H // 16]))
+
+        def weave_w(h):
             cols = slice(h * H, (h + 1) * H)
-            copy(out=grouped[h][:, :, j0 : j0 + 2], in_=picked[:, j0 : j0 + 2, cols].rearrange("p j n -> p n j"))
+            nc.scalar.copy(out=w_woven[h][:, :, 0:2], in_=picked[:, :, cols].rearrange("p j n -> p n j"))
 
-        def weave_x(copy, c):
-            tile = keep.tile([P, C, PACK], BF16, name="x_grouped%d" % c, tag="woven%d" % (c % 2), align_bytes=512)
-            x_grouped.setdefault(c, tile)
-            copy(
-                out=tile[:].rearrange("p (c i) j -> p c j i", i=4),
-                in_=x_raw[c][:].rearrange("p j (c i) -> p c j i", i=4),
-            )
+        def woven_piece(c):
+            return sbuf("x_woven%d" % c, [P, C, PACK], BF16, slot="woven%d" % (c % 2))
 
-        def quantise(codes_t, scales_t, grouped_t):
-            nc.vector.quantize_mx(
-                out=codes_t.bitcast(FP8X4), scales=scales_t, in_=grouped_t.rearrange("p n j -> p (n j)")
-            )
+        def weave_x(copy, woven, raw):
+            copy(out=woven.rearrange("p (c i) j -> p c j i", i=4), in_=raw.rearrange("p j (c i) -> p c j i", i=4))
 
-        def quantise_x(c):
-            quantise(x_codes[c], x_scales[c][:], x_grouped[c][:])
+        def quantise(codes, scales, woven):
+            nc.vector.quantize_mx(out=codes.bitcast(FP8X4), scales=scales, in_=woven.rearrange("p n j -> p (n j)"))
 
         def quantise_w(q):
-            quantise(codes[q], scales[q][:], grouped[q // 2][:, (q % 2) * P : (q % 2 + 1) * P, :])
+            quantise(w_codes[q], w_scales[q][:], w_woven[q // 2][:, q % 2 * P : (q % 2 + 1) * P, :])
 
         def multiply(q, c):
             acc = psum.tile([P, C], F32, name="acc", tag="bank")
             nc.tensor.matmul_mx(
                 out=acc[:],
-                lhsT=codes[q].bitcast(FP8X4),
-                lhsT_scale=scales[q][:],
+                lhsT=w_codes[q].bitcast(FP8X4),
+                lhsT_scale=w_scales[q][:],
                 rhs=x_codes[c].bitcast(FP8X4),
                 rhs_scale=x_scales[c][:],
                 start=True,
                 stop=True,
             )
-            return acc
+            return acc[:]
 
-        def store_block(q, c):
-            nc.sync.dma_start(out_rows[:, q, c * C : (c + 1) * C], results[(q // 2, c)][:, q % 2, :])
+        def finish_scalar(result, q, c):
+            nc.scalar.activation(result, multiply(q, c), RELU, bias=bias[:, q : q + 1])
 
-        def result(q, c):
-            key = (q // 2, c)
-            if key not in results:
-                tag = RESULT_SLOTS.get(key, "result%d_%d" % key)
-                results.setdefault(key, keep.tile([P, 2, C], F32, name="result%d_%d" % key, tag=tag, align_bytes=512))
-            return results[key][:, q % 2, :]
+        def finish_vector(result, q, c):
+            nc.vector.tensor_scalar(result, multiply(q, c), bias[:, q : q + 1], 0.0, op0=ADD, op1=MAX)
 
-        def finish_scalar(q, c):
-            nc.scalar.activation(result(q, c), multiply(q, c)[:], RELU, bias=bias[:, q : q + 1])
-
-        def finish_vector(q, c):
-            nc.vector.tensor_scalar(
-                result(q, c), multiply(q, c)[:], bias[:, q : q + 1], 0.0, op0=ADD, op1=MAX
-            )
-
-        def store(h, c):
-            nc.sync.dma_start(out_rows[:, 2 * h : 2 * h + 2, c * C : (c + 1) * C], results[(h, c)][:])
-
-        def gather(h, j, window):
-            nc.vector.tensor_copy(grouped[h][:, :, j], window.indirect(lists[:, h * H // 16 : (h + 1) * H // 16]))
+        def finish_pair(first, c, finishers, one_by_one, slot=None):
+            pair = sbuf("result%d_%d" % (first, c), [P, 2, C], F32, slot=slot)
+            tokens = slice(c * C, (c + 1) * C)
+            for r, finish in enumerate(finishers):
+                finish(pair[:, r, :], first + r, c)
+                if one_by_one:
+                    nc.sync.dma_start(out_rows[:, first + r, tokens], pair[:, r, :])
+            if not one_by_one:
+                nc.sync.dma_start(out_rows[:, first : first + 2, tokens], pair[:])
 
         for j in range(2):
-            nc.vector.tensor_copy(picked[:, j, :], planes[j].indirect(lists[:]))
+            nc.vector.tensor_copy(picked[:, j, :], planes01[:, j, :].indirect(lists[:]))
         for h in range(2):
-            weave(nc.scalar.copy, h, 0)
-            gather(h, 2, planes[2])
-        gather(0, 3, planes[3][:, 0:FIRST])
-        weave_x(nc.scalar.copy, 0)
-        nc.scalar.copy(out=bias[:], in_=turned[:, 0:4])
-        gather(1, 3, planes[3])
-        weave_x(nc.scalar.copy, 1)
+            weave_w(h)
+            gather(h, 2, plane2[:])
+        gather(0, 3, plane3[:, 0:FIRST])
+        woven0 = woven_piece(0)
+        weave_x(nc.scalar.copy, woven0[:], x_raw[0][:])
+        nc.scalar.copy(out=bias[:], in_=turned[:, 0:BLOCKS])
+        gather(1, 3, plane3[:])
+        woven1 = woven_piece(1)
+        weave_x(nc.scalar.copy, woven1[:], x_raw[1][:])
         quantise_w(0)
-        quantise_x(0)
-        quantise_w(1)
-        quantise_w(2)
-        quantise_w(3)
-        quantise_x(1)
-        weave_x(nc.vector.tensor_copy, 2)
-        weave_x(nc.vector.tensor_copy, 3)
-        quantise_x(2)
-        quantise_x(3)
-        finish_scalar(0, 0)
-        store_block(0, 0)
-        finish_scalar(1, 0)
-        store_block(1, 0)
-        finish_scalar(2, 0)
-        finish_scalar(3, 0)
-        store(1, 0)
-        finish_scalar(0, 1)
-        finish_scalar(1, 1)
-        store(0, 1)
-        finish_scalar(2, 1)
-        finish_scalar(3, 1)
-        store(1, 1)
-        finish_scalar(0, 2)
-        finish_vector(2, 2)
-        finish_scalar(1, 2)
-        store(0, 2)
-        finish_vector(3, 2)
-        store(1, 2)
-        finish_scalar(0, 3)
-        finish_vector(1, 3)
-        store(0, 3)
-        finish_scalar(2, 3)
-        finish_vector(3, 3)
-        store(1, 3)
+        quantise(x_codes[0], x_scales[0][:], woven0[:])
+        for q in range(1, BLOCKS):
+            quantise_w(q)
+        quantise(x_codes[1], x_scales[1][:], woven1[:])
+
+        halves = (slice(0, C // 2), slice(C // 2, C))
+        woven2 = woven_piece(2)
+        weave_x(nc.vector.tensor_copy, woven2[:], x_raw[2][:, :, 0:C])
+        woven3 = woven_piece(3)
+        weave_x(nc.vector.tensor_copy, woven3[:, halves[0], :], x_raw[2][:, :, C:])
+        quantise(x_codes[2], x_scales[2][:], woven2[:])
+        weave_x(nc.vector.tensor_copy, woven3[:, halves[1], :], x_raw[3][:])
+        for half in halves:
+            quantise(x_codes[3][:, half], x_scales[3][:, half], woven3[:, half, :])
+
+        for c in range(2):
+            finish_pair(0, c, (finish_scalar, finish_scalar), True)
+            finish_pair(2, c, (finish_scalar, finish_scalar), False)
+        finish_pair(0, 2, (finish_scalar, finish_scalar), True)
+        finish_pair(2, 2, (finish_vector, finish_vector), False, slot="woven1")
+        for first in (0, 2):
+            finish_pair(first, 3, (finish_scalar, finish_vector), False)

@@ -9,6 +9,7 @@ FLOPS = 2 * K * S * T
 F32 = mybir.dt.float32
 BF16 = mybir.dt.bfloat16
 U32 = mybir.dt.uint32
+I32 = mybir.dt.int32
 U16 = mybir.dt.uint16
 U8 = mybir.dt.uint8
 FP8X4 = mybir.dt.float8_e4m3fn_x4
@@ -28,10 +29,14 @@ def tile_picked_neuron_lin_relu_srt_e_kernel(tc, w, xT, b, offs, out):
     nc = tc.nc
     with ExitStack() as ctx:
         keep = ctx.enter_context(tc.tile_pool(name="keep", bufs=1))
+        held = ctx.enter_context(tc.tile_pool(name="held", bufs=1))
         psum = ctx.enter_context(tc.psum_pool(name="psum", bufs=8))
 
         def sbuf(name, shape, dtype, slot=None):
             return keep.tile(shape, dtype, name=name, tag=slot or name, align_bytes=ALIGN)
+
+        def placed(name, shape, dtype, offset):
+            return held.tile(shape, dtype, name=name, tag=name, align_bytes=ALIGN, offset=offset)
 
         w_rows = w.rearrange("(p j) n -> p j n", j=PACK)
         x_rows = xT.rearrange("(p j) t -> p j t", j=PACK)
@@ -43,9 +48,9 @@ def tile_picked_neuron_lin_relu_srt_e_kernel(tc, w, xT, b, offs, out):
         plane2 = sbuf("plane2", [P, N], F32)
         plane3 = sbuf("plane3", [P, N], F32)
         x_raw = [sbuf("x_raw%d" % n, [P, PACK, x_cuts[n + 1] - x_cuts[n]], F32) for n in range(4)]
-        b_rows = sbuf("b_rows", [P, P], F32)
+        b_rows = placed("b_rows", [P, P], F32, 768)
         bias = sbuf("bias", [P, BLOCKS], F32)
-        identity = sbuf("identity", [P, P], F32)
+        identity = placed("identity", [P, P], F32, 3328)
 
         def load_x(n, planes_at_once):
             for j in range(0, PACK, planes_at_once):
@@ -59,28 +64,35 @@ def tile_picked_neuron_lin_relu_srt_e_kernel(tc, w, xT, b, offs, out):
         nc.sync.dma_start(plane2[:], w_rows[:, 2, :])
         nc.sync.dma_start(plane3[:, 0:FIRST], w_rows[:, 3, 0:FIRST])
         nc.sync.dma_start(plane3[:, FIRST:N], w_rows[:, 3, FIRST:N])
-        load_x(0, PACK)
         nc.sync.dma_start(b_rows[0:BLOCKS, :], b.rearrange("(q i) o -> q (i o)", q=BLOCKS))
+        load_x(0, PACK)
         load_x(1, PACK)
         load_x(2, 2)
         load_x(3, 2)
         turned = psum.tile([P, P], F32, name="turned", tag="bank")
         nc.tensor.transpose(turned[:], b_rows[:], identity[:])
 
-        picked = sbuf("picked", [P, 2, S], F32)
-        w_woven = [sbuf("w_woven%d" % h, [P, H, PACK], BF16) for h in range(2)]
-        held = sbuf("held", [P, S + C], U32, slot="b_rows")
-        w_codes = [held[:, q * P : (q + 1) * P] for q in range(BLOCKS)]
-        w_scales = [sbuf("w_scales%d" % q, [P, P], U8) for q in range(BLOCKS)]
-        x_codes = [held[:, S:]] + [sbuf("x_codes%d" % c, [P, C], U32)[:] for c in range(1, 4)]
+        pairs = [sbuf("pairs%d" % h, [P, 2, H, 2], BF16) for h in range(2)]
+        w_woven0 = sbuf("w_woven0", [P, P, PACK], BF16)
+        w_woven1 = placed("w_woven1", [P, P, PACK], BF16, 0)
+        w_woven23 = placed("w_woven23", [P, H, PACK], BF16, 1536)
+        w_codes0 = placed("w_codes0", [P, P], U32, 1024)
+        w_codes1 = placed("w_codes1", [P, P], U32, 3584)
+        w_codes23 = sbuf("w_codes23", [P, H], U32, slot="x_raw0")
+        w_codes = [w_codes0[:], w_codes1[:], w_codes23[:, 0:P], w_codes23[:, P:H]]
+        w_scales01 = [sbuf("w_scales%d" % q, [P, P], U8) for q in range(2)]
+        w_scales23 = sbuf("w_scales23", [P, H], U8)
+        w_scales = [w_scales01[0][:], w_scales01[1][:], w_scales23[:, 0:P], w_scales23[:, P:H]]
+        x_codes = [sbuf("x_codes%d" % c, [P, C], U32)[:] for c in range(4)]
         x_scales = [sbuf("x_scales%d" % c, [P, C], U8) for c in range(4)]
 
         def gather(h, j, window):
-            nc.vector.tensor_copy(w_woven[h][:, :, j], window.indirect(lists[:, h * H // 16 : (h + 1) * H // 16]))
+            nc.vector.tensor_copy(pairs[h][:, j // 2, :, j % 2], window.indirect(lists[:, h * H // 16 : (h + 1) * H // 16]))
 
-        def weave_w(h):
-            cols = slice(h * H, (h + 1) * H)
-            nc.scalar.copy(out=w_woven[h][:, :, 0:2], in_=picked[:, :, cols].rearrange("p j n -> p n j"))
+        def weave_w(copy, word, woven, h, cols):
+            words = pairs[h][:].rearrange("p u n e -> p u (n e)").bitcast(word)[:, :, cols]
+            woven_words = woven.rearrange("p n j -> p (n j)").bitcast(word)
+            copy(out=woven_words.rearrange("p (n u) -> p n u", u=2), in_=words.rearrange("p u n -> p n u"))
 
         def woven_piece(c):
             return sbuf("x_woven%d" % c, [P, C, PACK], BF16, slot="woven%d" % (c % 2))
@@ -91,15 +103,12 @@ def tile_picked_neuron_lin_relu_srt_e_kernel(tc, w, xT, b, offs, out):
         def quantise(codes, scales, woven):
             nc.vector.quantize_mx(out=codes.bitcast(FP8X4), scales=scales, in_=woven.rearrange("p n j -> p (n j)"))
 
-        def quantise_w(q):
-            quantise(w_codes[q], w_scales[q][:], w_woven[q // 2][:, q % 2 * P : (q % 2 + 1) * P, :])
-
         def multiply(q, c):
             acc = psum.tile([P, C], F32, name="acc", tag="bank")
             nc.tensor.matmul_mx(
                 out=acc[:],
                 lhsT=w_codes[q].bitcast(FP8X4),
-                lhsT_scale=w_scales[q][:],
+                lhsT_scale=w_scales[q],
                 rhs=x_codes[c].bitcast(FP8X4),
                 rhs_scale=x_scales[c][:],
                 start=True,
@@ -123,22 +132,25 @@ def tile_picked_neuron_lin_relu_srt_e_kernel(tc, w, xT, b, offs, out):
             if not one_by_one:
                 nc.sync.dma_start(out_rows[:, first : first + 2, tokens], pair[:])
 
-        for j in range(2):
-            nc.vector.tensor_copy(picked[:, j, :], planes01[:, j, :].indirect(lists[:]))
         for h in range(2):
-            weave_w(h)
+            for j in range(2):
+                gather(h, j, planes01[:, j, :])
+        for h in range(2):
             gather(h, 2, plane2[:])
         gather(0, 3, plane3[:, 0:FIRST])
+        weave_w(nc.scalar.copy, U32, w_woven0[:], 0, slice(0, P))
+        gather(1, 3, plane3[:])
+        nc.scalar.copy(out=bias[:], in_=turned[:, 0:BLOCKS])
         woven0 = woven_piece(0)
         weave_x(nc.scalar.copy, woven0[:], x_raw[0][:])
-        nc.scalar.copy(out=bias[:], in_=turned[:, 0:BLOCKS])
-        gather(1, 3, plane3[:])
         woven1 = woven_piece(1)
         weave_x(nc.scalar.copy, woven1[:], x_raw[1][:])
-        quantise_w(0)
+        weave_w(nc.vector.tensor_copy, I32, w_woven1[:], 0, slice(P, H))
+        weave_w(nc.vector.tensor_copy, I32, w_woven23[:], 1, slice(0, H))
+        quantise(w_codes[0], w_scales[0], w_woven0[:])
+        quantise(w_codes[1], w_scales[1], w_woven1[:])
         quantise(x_codes[0], x_scales[0][:], woven0[:])
-        for q in range(1, BLOCKS):
-            quantise_w(q)
+        quantise(w_codes23[:], w_scales23[:], w_woven23[:])
         quantise(x_codes[1], x_scales[1][:], woven1[:])
 
         halves = (slice(0, C // 2), slice(C // 2, C))

@@ -9,19 +9,18 @@ FLOPS = 2 * K * S * T
 F32 = mybir.dt.float32
 BF16 = mybir.dt.bfloat16
 U32 = mybir.dt.uint32
-I32 = mybir.dt.int32
 U16 = mybir.dt.uint16
 U8 = mybir.dt.uint8
 FP8X4 = mybir.dt.float8_e4m3fn_x4
 ADD, MAX = mybir.AluOpType.add, mybir.AluOpType.max
 RELU = mybir.ActivationFunctionType.Relu
+COPY = mybir.ActivationFunctionType.Copy
 
 P = 128
 PACK = 4
 BLOCKS = S // P
-H = S // 2
 C = 128
-FIRST = N - H
+PIECES = T // C
 ALIGN = 256
 
 
@@ -29,144 +28,136 @@ def tile_picked_neuron_lin_relu_srt_e_kernel(tc, w, xT, b, offs, out):
     nc = tc.nc
     with ExitStack() as ctx:
         keep = ctx.enter_context(tc.tile_pool(name="keep", bufs=1))
-        held = ctx.enter_context(tc.tile_pool(name="held", bufs=1))
         psum = ctx.enter_context(tc.psum_pool(name="psum", bufs=8))
 
         def sbuf(name, shape, dtype, slot=None):
             return keep.tile(shape, dtype, name=name, tag=slot or name, align_bytes=ALIGN)
 
-        def placed(name, shape, dtype, offset):
-            return held.tile(shape, dtype, name=name, tag=name, align_bytes=ALIGN, offset=offset)
-
         w_rows = w.rearrange("(p j) n -> p j n", j=PACK)
         x_rows = xT.rearrange("(p j) t -> p j t", j=PACK)
         out_rows = out.rearrange("(q p) t -> p q t", p=P)
 
-        x_cuts = (0, C, 2 * C, T - C // 2, T)
         lists = sbuf("lists", [P, S // 16], U16)
         planes01 = sbuf("planes01", [P, 2, N], F32)
         plane2 = sbuf("plane2", [P, N], F32)
         plane3 = sbuf("plane3", [P, N], F32)
-        x_raw = [sbuf("x_raw%d" % n, [P, PACK, x_cuts[n + 1] - x_cuts[n]], F32) for n in range(4)]
-        b_rows = placed("b_rows", [P, P], F32, 768)
+        x_raw0 = sbuf("x_raw0", [P, PACK, C], F32)
+        x_raw1 = sbuf("x_raw1", [P, PACK, C], F32)
+        x_raw23 = sbuf("x_raw23", [P, PACK, 2 * C], F32)
+        x_raw = [x_raw0[:], x_raw1[:], x_raw23[:, :, 0:C], x_raw23[:, :, C : 2 * C]]
+        b_rows = sbuf("b_rows", [P, P], F32)
         bias = sbuf("bias", [P, BLOCKS], F32)
-        identity = placed("identity", [P, P], F32, 3328)
+        identity = sbuf("identity", [P, P], F32)
 
-        def load_x(n, planes_at_once):
-            for j in range(0, PACK, planes_at_once):
-                rows = slice(j, j + planes_at_once)
-                nc.sync.dma_start(x_raw[n][:, rows, :], x_rows[:, rows, x_cuts[n] : x_cuts[n + 1]])
-
-        nc.vector.memset(b_rows[:], 0.0)
+        nc.vector.memset(b_rows[:, 0 : P // 2], 0.0)
+        nc.scalar.activation(b_rows[:, P // 2 : P], b_rows[:, 0 : P // 2], COPY)
         make_identity(nc, identity[:])
         nc.sync.dma_start(planes01[:], w_rows[:, 0:2, :])
         nc.sync.dma_start(lists[:], offs)
-        nc.sync.dma_start(plane2[:], w_rows[:, 2, :])
-        nc.sync.dma_start(plane3[:, 0:FIRST], w_rows[:, 3, 0:FIRST])
-        nc.sync.dma_start(plane3[:, FIRST:N], w_rows[:, 3, FIRST:N])
         nc.sync.dma_start(b_rows[0:BLOCKS, :], b.rearrange("(q i) o -> q (i o)", q=BLOCKS))
-        load_x(0, PACK)
-        load_x(1, PACK)
-        load_x(2, 2)
-        load_x(3, 2)
+        nc.sync.dma_start(plane2[:], w_rows[:, 2, :])
+        nc.sync.dma_start(plane3[:], w_rows[:, 3, :])
+        nc.sync.dma_start(x_raw0[:], x_rows[:, :, 0:C])
+        nc.sync.dma_start(x_raw1[:], x_rows[:, :, C : 2 * C])
+        nc.sync.dma_start(x_raw23[:], x_rows[:, :, 2 * C : T])
         turned = psum.tile([P, P], F32, name="turned", tag="bank")
         nc.tensor.transpose(turned[:], b_rows[:], identity[:])
 
-        pairs = [sbuf("pairs%d" % h, [P, 2, H, 2], BF16) for h in range(2)]
-        w_woven0 = sbuf("w_woven0", [P, P, PACK], BF16)
-        w_woven1 = placed("w_woven1", [P, P, PACK], BF16, 0)
-        w_woven23 = placed("w_woven23", [P, H, PACK], BF16, 1536)
-        w_codes0 = placed("w_codes0", [P, P], U32, 1024)
-        w_codes1 = placed("w_codes1", [P, P], U32, 3584)
-        w_codes23 = sbuf("w_codes23", [P, H], U32, slot="x_raw0")
-        w_codes = [w_codes0[:], w_codes1[:], w_codes23[:, 0:P], w_codes23[:, P:H]]
-        w_scales01 = [sbuf("w_scales%d" % q, [P, P], U8) for q in range(2)]
-        w_scales23 = sbuf("w_scales23", [P, H], U8)
-        w_scales = [w_scales01[0][:], w_scales01[1][:], w_scales23[:, 0:P], w_scales23[:, P:H]]
-        x_codes = [sbuf("x_codes%d" % c, [P, C], U32)[:] for c in range(4)]
-        x_scales = [sbuf("x_scales%d" % c, [P, C], U8) for c in range(4)]
+        picked01 = sbuf("picked01", [P, 2, S], F32)
+        picked2 = [sbuf("picked2_%d" % h, [P, 2 * P], BF16) for h in range(2)]
+        picked3 = [sbuf("picked3_%d" % q, [P, P], BF16) for q in range(BLOCKS)]
+        w_woven = [sbuf("w_woven%d" % q, [P, P, PACK], BF16) for q in range(BLOCKS)]
+        w_codes0 = sbuf("w_codes0", [P, P], U32)
+        w_codes123 = sbuf("w_codes123", [P, BLOCKS - 1, P], U32, slot="x_raw0")
+        w_codes = [w_codes0[:]] + [w_codes123[:, q, :] for q in range(BLOCKS - 1)]
+        w_scales = [sbuf("w_scales%d" % q, [P, P], U8) for q in range(BLOCKS)]
+        x_woven = [sbuf("x_woven%d" % c, [P, C, PACK], BF16) for c in range(PIECES)]
+        x_codes = sbuf("x_codes", [P, T], U32)
+        x_scales = sbuf("x_scales", [P, T], U8)
 
-        def gather(h, j, window):
-            nc.vector.tensor_copy(pairs[h][:, j // 2, :, j % 2], window.indirect(lists[:, h * H // 16 : (h + 1) * H // 16]))
+        def looked_up(window, first, count):
+            return window.indirect(lists[:, first // 16 : (first + count) // 16])
 
-        def weave_w(copy, word, woven, h, cols):
-            words = pairs[h][:].rearrange("p u n e -> p u (n e)").bitcast(word)[:, :, cols]
-            woven_words = woven.rearrange("p n j -> p (n j)").bitcast(word)
-            copy(out=woven_words.rearrange("p (n u) -> p n u", u=2), in_=words.rearrange("p u n -> p n u"))
+        def gather_vector(picked, window, first, count):
+            nc.vector.tensor_copy(picked, looked_up(window, first, count))
 
-        def woven_piece(c):
-            return sbuf("x_woven%d" % c, [P, C, PACK], BF16, slot="woven%d" % (c % 2))
+        def gather_scalar(picked, window, first, count):
+            nc.scalar.activation(picked, looked_up(window, first, count), COPY)
 
-        def weave_x(copy, woven, raw):
-            copy(out=woven.rearrange("p (c i) j -> p c j i", i=4), in_=raw.rearrange("p j (c i) -> p c j i", i=4))
+        def insert(q, j, picked):
+            nc.vector.tensor_copy(w_woven[q][:, :, j], picked)
+
+        def weave_x(copy, c, tokens):
+            copy(
+                out=x_woven[c][:, tokens, :].rearrange("p (c i) j -> p c j i", i=4),
+                in_=x_raw[c][:, :, tokens].rearrange("p j (c i) -> p c j i", i=4),
+            )
 
         def quantise(codes, scales, woven):
             nc.vector.quantize_mx(out=codes.bitcast(FP8X4), scales=scales, in_=woven.rearrange("p n j -> p (n j)"))
 
-        def multiply(q, c):
-            acc = psum.tile([P, C], F32, name="acc", tag="bank")
+        def quantise_w(q):
+            quantise(w_codes[q], w_scales[q][:], w_woven[q][:])
+
+        def quantise_x(c):
+            tokens = slice(c * C, (c + 1) * C)
+            quantise(x_codes[:, tokens], x_scales[:, tokens], x_woven[c][:])
+
+        def multiply(q, tokens):
+            acc = psum.tile([P, tokens.stop - tokens.start], F32, name="acc", tag="bank")
             nc.tensor.matmul_mx(
                 out=acc[:],
                 lhsT=w_codes[q].bitcast(FP8X4),
-                lhsT_scale=w_scales[q],
-                rhs=x_codes[c].bitcast(FP8X4),
-                rhs_scale=x_scales[c][:],
+                lhsT_scale=w_scales[q][:],
+                rhs=x_codes[:, tokens].bitcast(FP8X4),
+                rhs_scale=x_scales[:, tokens],
                 start=True,
                 stop=True,
             )
             return acc[:]
 
-        def finish_scalar(result, q, c):
-            nc.scalar.activation(result, multiply(q, c), RELU, bias=bias[:, q : q + 1])
+        def finish_scalar(result, q, tokens):
+            nc.scalar.activation(result, multiply(q, tokens), RELU, bias=bias[:, q : q + 1])
 
-        def finish_vector(result, q, c):
-            nc.vector.tensor_scalar(result, multiply(q, c), bias[:, q : q + 1], 0.0, op0=ADD, op1=MAX)
+        def finish_vector(result, q, tokens):
+            nc.vector.tensor_scalar(result, multiply(q, tokens), bias[:, q : q + 1], 0.0, op0=ADD, op1=MAX)
 
-        def finish_pair(first, c, finishers, one_by_one, slot=None):
-            pair = sbuf("result%d_%d" % (first, c), [P, 2, C], F32, slot=slot)
-            tokens = slice(c * C, (c + 1) * C)
+        def finish_pair(first, tokens, finishers):
+            pair = sbuf("result%d_%d" % (first, tokens.start), [P, 2, tokens.stop - tokens.start], F32)
             for r, finish in enumerate(finishers):
-                finish(pair[:, r, :], first + r, c)
-                if one_by_one:
-                    nc.sync.dma_start(out_rows[:, first + r, tokens], pair[:, r, :])
-            if not one_by_one:
-                nc.sync.dma_start(out_rows[:, first : first + 2, tokens], pair[:])
+                finish(pair[:, r, :], first + r, tokens)
+            nc.sync.dma_start(out_rows[:, first : first + 2, tokens], pair[:])
 
-        for h in range(2):
-            for j in range(2):
-                gather(h, j, planes01[:, j, :])
-        for h in range(2):
-            gather(h, 2, plane2[:])
-        gather(0, 3, plane3[:, 0:FIRST])
-        weave_w(nc.scalar.copy, U32, w_woven0[:], 0, slice(0, P))
-        gather(1, 3, plane3[:])
+        gather_vector(picked01[:, 0, :], planes01[:, 0, :], 0, S)
+        gather_scalar(picked01[:, 1, :], planes01[:, 1, :], 0, S)
         nc.scalar.copy(out=bias[:], in_=turned[:, 0:BLOCKS])
-        woven0 = woven_piece(0)
-        weave_x(nc.scalar.copy, woven0[:], x_raw[0][:])
-        woven1 = woven_piece(1)
-        weave_x(nc.scalar.copy, woven1[:], x_raw[1][:])
-        weave_w(nc.vector.tensor_copy, I32, w_woven1[:], 0, slice(P, H))
-        weave_w(nc.vector.tensor_copy, I32, w_woven23[:], 1, slice(0, H))
-        quantise(w_codes[0], w_scales[0], w_woven0[:])
-        quantise(w_codes[1], w_scales[1], w_woven1[:])
-        quantise(x_codes[0], x_scales[0][:], woven0[:])
-        quantise(w_codes23[:], w_scales23[:], w_woven23[:])
-        quantise(x_codes[1], x_scales[1][:], woven1[:])
+        for q in range(BLOCKS):
+            nc.vector.tensor_copy(w_woven[q][:, :, 0:2], picked01[:, :, q * P : (q + 1) * P].rearrange("p j n -> p n j"))
+        gather_vector(picked2[0][:], plane2[:], 0, 2 * P)
+        gather_scalar(picked2[1][:], plane2[:], 2 * P, 2 * P)
+        for q in range(BLOCKS):
+            insert(q, 2, picked2[q // 2][:, (q % 2) * P : (q % 2 + 1) * P])
 
-        halves = (slice(0, C // 2), slice(C // 2, C))
-        woven2 = woven_piece(2)
-        weave_x(nc.vector.tensor_copy, woven2[:], x_raw[2][:, :, 0:C])
-        woven3 = woven_piece(3)
-        weave_x(nc.vector.tensor_copy, woven3[:, halves[0], :], x_raw[2][:, :, C:])
-        quantise(x_codes[2], x_scales[2][:], woven2[:])
-        weave_x(nc.vector.tensor_copy, woven3[:, halves[1], :], x_raw[3][:])
-        for half in halves:
-            quantise(x_codes[3][:, half], x_scales[3][:, half], woven3[:, half, :])
+        for q in range(BLOCKS):
+            (gather_vector, gather_scalar)[q % 2](picked3[q][:], plane3[:], q * P, P)
+        for q in range(BLOCKS):
+            insert(q, 3, picked3[q][:])
+        weave_x(nc.scalar.copy, 0, slice(0, C))
+        weave_x(nc.scalar.copy, 1, slice(0, C))
+        quantise_w(0)
+        quantise_x(0)
+        for q in range(1, BLOCKS):
+            quantise_w(q)
+        quantise_x(1)
+        weave_x(nc.vector.tensor_copy, 2, slice(0, C))
+        weave_x(nc.vector.tensor_copy, 3, slice(0, C))
+        quantise_x(2)
+        quantise_x(3)
 
-        for c in range(2):
-            finish_pair(0, c, (finish_scalar, finish_scalar), True)
-            finish_pair(2, c, (finish_scalar, finish_scalar), False)
-        finish_pair(0, 2, (finish_scalar, finish_scalar), True)
-        finish_pair(2, 2, (finish_vector, finish_vector), False, slot="woven1")
-        for first in (0, 2):
-            finish_pair(first, 3, (finish_scalar, finish_vector), False)
+        both_scalar = (finish_scalar, finish_scalar)
+        for c in (0, 1):
+            for first in (0, 2):
+                finish_pair(first, slice(c * C, (c + 1) * C), both_scalar)
+        for c in (2, 3):
+            for first in (0, 2):
+                finish_pair(first, slice(c * C, (c + 1) * C), (finish_scalar, finish_vector))

@@ -22,6 +22,7 @@ BLOCKS = S // P
 C = 128
 PIECES = T // C
 ALIGN = 256
+SHARE = 96
 
 
 def tile_picked_neuron_lin_relu_srt_e_kernel(tc, w, xT, b, offs, out):
@@ -41,10 +42,7 @@ def tile_picked_neuron_lin_relu_srt_e_kernel(tc, w, xT, b, offs, out):
         planes01 = sbuf("planes01", [P, 2, N], F32)
         plane2 = sbuf("plane2", [P, N], F32)
         plane3 = sbuf("plane3", [P, N], F32)
-        x_raw0 = sbuf("x_raw0", [P, PACK, C], F32)
-        x_raw1 = sbuf("x_raw1", [P, PACK, C], F32)
-        x_raw23 = sbuf("x_raw23", [P, PACK, 2 * C], F32)
-        x_raw = [x_raw0[:], x_raw1[:], x_raw23[:, :, 0:C], x_raw23[:, :, C : 2 * C]]
+        x_raw = [sbuf("x_raw%d" % c, [P, PACK, C], F32) for c in range(PIECES)]
         b_rows = sbuf("b_rows", [P, P], F32)
         bias = sbuf("bias", [P, BLOCKS], F32)
         identity = sbuf("identity", [P, P], F32)
@@ -57,15 +55,13 @@ def tile_picked_neuron_lin_relu_srt_e_kernel(tc, w, xT, b, offs, out):
         nc.sync.dma_start(b_rows[0:BLOCKS, :], b.rearrange("(q i) o -> q (i o)", q=BLOCKS))
         nc.sync.dma_start(plane2[:], w_rows[:, 2, :])
         nc.sync.dma_start(plane3[:], w_rows[:, 3, :])
-        nc.sync.dma_start(x_raw0[:], x_rows[:, :, 0:C])
-        nc.sync.dma_start(x_raw1[:], x_rows[:, :, C : 2 * C])
-        nc.sync.dma_start(x_raw23[:], x_rows[:, :, 2 * C : T])
+        for c in range(PIECES):
+            nc.sync.dma_start(x_raw[c][:], x_rows[:, :, c * C : (c + 1) * C])
         turned = psum.tile([P, P], F32, name="turned", tag="bank")
         nc.tensor.transpose(turned[:], b_rows[:], identity[:])
 
         picked01 = sbuf("picked01", [P, 2, S], F32)
-        picked2 = [sbuf("picked2_%d" % h, [P, 2 * P], BF16) for h in range(2)]
-        picked3 = [sbuf("picked3_%d" % q, [P, P], BF16) for q in range(BLOCKS)]
+        picked23 = sbuf("picked23", [P, 2, S], BF16)
         w_woven = [sbuf("w_woven%d" % q, [P, P, PACK], BF16) for q in range(BLOCKS)]
         w_codes0 = sbuf("w_codes0", [P, P], U32)
         w_codes123 = sbuf("w_codes123", [P, BLOCKS - 1, P], U32, slot="x_raw0")
@@ -85,7 +81,7 @@ def tile_picked_neuron_lin_relu_srt_e_kernel(tc, w, xT, b, offs, out):
             nc.scalar.activation(picked, looked_up(window, first, count), COPY)
 
         def insert(q, j, picked):
-            nc.vector.tensor_copy(w_woven[q][:, :, j], picked)
+            nc.vector.tensor_copy(w_woven[q][:, :, j : j + 2], picked[:, :, q * P : (q + 1) * P].rearrange("p j n -> p n j"))
 
         def weave_x(copy, c, tokens):
             copy(
@@ -122,42 +118,42 @@ def tile_picked_neuron_lin_relu_srt_e_kernel(tc, w, xT, b, offs, out):
         def finish_vector(result, q, tokens):
             nc.vector.tensor_scalar(result, multiply(q, tokens), bias[:, q : q + 1], 0.0, op0=ADD, op1=MAX)
 
-        def finish_pair(first, tokens, finishers):
-            pair = sbuf("result%d_%d" % (first, tokens.start), [P, 2, tokens.stop - tokens.start], F32)
-            for r, finish in enumerate(finishers):
-                finish(pair[:, r, :], first + r, tokens)
-            nc.sync.dma_start(out_rows[:, first : first + 2, tokens], pair[:])
+        def finish(c, first, finishers, blocks_a_store, slot=None):
+            result = sbuf("result%d_%d" % (c, first), [P, len(finishers), C], F32, slot=slot)
+            tokens = slice(c * C, (c + 1) * C)
+            for r, finisher in enumerate(finishers):
+                finisher(result[:, r, :], first + r, tokens)
+                if (r + 1) % blocks_a_store == 0:
+                    low = r + 1 - blocks_a_store
+                    nc.sync.dma_start(out_rows[:, first + low : first + r + 1, tokens], result[:, low : r + 1, :])
 
         gather_vector(picked01[:, 0, :], planes01[:, 0, :], 0, S)
         gather_scalar(picked01[:, 1, :], planes01[:, 1, :], 0, S)
         nc.scalar.copy(out=bias[:], in_=turned[:, 0:BLOCKS])
         for q in range(BLOCKS):
-            nc.vector.tensor_copy(w_woven[q][:, :, 0:2], picked01[:, :, q * P : (q + 1) * P].rearrange("p j n -> p n j"))
-        gather_vector(picked2[0][:], plane2[:], 0, 2 * P)
-        gather_scalar(picked2[1][:], plane2[:], 2 * P, 2 * P)
-        for q in range(BLOCKS):
-            insert(q, 2, picked2[q // 2][:, (q % 2) * P : (q % 2 + 1) * P])
+            insert(q, 0, picked01)
+        gather_vector(picked23[:, 0, 0 : 2 * P], plane2[:], 0, 2 * P)
+        gather_scalar(picked23[:, 0, 2 * P : S], plane2[:], 2 * P, 2 * P)
 
         for q in range(BLOCKS):
-            (gather_vector, gather_scalar)[q % 2](picked3[q][:], plane3[:], q * P, P)
+            (gather_vector, gather_scalar)[q % 2](picked23[:, 1, q * P : (q + 1) * P], plane3[:], q * P, P)
         for q in range(BLOCKS):
-            insert(q, 3, picked3[q][:])
+            insert(q, 2, picked23)
         weave_x(nc.scalar.copy, 0, slice(0, C))
         weave_x(nc.scalar.copy, 1, slice(0, C))
+        weave_x(nc.scalar.copy, 2, slice(0, SHARE))
         quantise_w(0)
         quantise_x(0)
         for q in range(1, BLOCKS):
             quantise_w(q)
         quantise_x(1)
-        weave_x(nc.vector.tensor_copy, 2, slice(0, C))
+        weave_x(nc.vector.tensor_copy, 2, slice(SHARE, C))
         weave_x(nc.vector.tensor_copy, 3, slice(0, C))
         quantise_x(2)
         quantise_x(3)
 
-        both_scalar = (finish_scalar, finish_scalar)
-        for c in (0, 1):
-            for first in (0, 2):
-                finish_pair(first, slice(c * C, (c + 1) * C), both_scalar)
+        finish(0, 0, (finish_scalar,) * BLOCKS, 2, slot="x_raw1")
+        finish(1, 0, (finish_scalar, finish_scalar), 2)
+        finish(1, 2, (finish_vector, finish_scalar), 2, slot="x_woven2")
         for c in (2, 3):
-            for first in (0, 2):
-                finish_pair(first, slice(c * C, (c + 1) * C), (finish_scalar, finish_vector))
+            finish(c, 0, (finish_scalar, finish_vector) * 2, BLOCKS)

@@ -155,5 +155,5 @@ def tile_picked_neuron_lin_relu_srt_e_kernel(tc, w, xT, b, offs, out):
         finish(0, 0, (finish_scalar,) * BLOCKS, 2, slot="x_raw1")
         finish(1, 0, (finish_scalar, finish_scalar), 2)
         finish(1, 2, (finish_vector, finish_scalar), 2, slot="x_woven2")
-        for c in (2, 3):
-            finish(c, 0, (finish_scalar, finish_vector) * 2, BLOCKS)
+        finish(2, 0, (finish_scalar, finish_vector) * 2, BLOCKS)
+        finish(3, 0, (finish_scalar, finish_vector) * 2, 2)

@@ -1,7 +1,6 @@
 from contextlib import ExitStack
 
 import concourse.mybir as mybir
-from concourse.masks import make_identity
 
 K, N, T, S = 512, 2048, 512, 512
 FLOPS = 2 * K * S * T
@@ -23,6 +22,7 @@ C = 128
 PIECES = T // C
 ALIGN = 256
 SHARE = 96
+SQUARE = 32
 
 
 def tile_picked_neuron_lin_relu_srt_e_kernel(tc, w, xT, b, offs, out):
@@ -44,21 +44,20 @@ def tile_picked_neuron_lin_relu_srt_e_kernel(tc, w, xT, b, offs, out):
         plane3 = sbuf("plane3", [P, N], F32)
         x_raw = [sbuf("x_raw%d" % c, [P, PACK, C], F32) for c in range(PIECES)]
         b_rows = sbuf("b_rows", [P, P], F32)
-        bias = sbuf("bias", [P, BLOCKS], F32)
-        identity = sbuf("identity", [P, P], F32)
+        turned = sbuf("turned", [P, P], F32)
 
         nc.vector.memset(b_rows[:, 0 : P // 2], 0.0)
         nc.scalar.activation(b_rows[:, P // 2 : P], b_rows[:, 0 : P // 2], COPY)
-        make_identity(nc, identity[:])
         nc.sync.dma_start(planes01[:], w_rows[:, 0:2, :])
         nc.sync.dma_start(lists[:], offs)
-        nc.sync.dma_start(b_rows[0:BLOCKS, :], b.rearrange("(q i) o -> q (i o)", q=BLOCKS))
+        nc.sync.dma_start(
+            b_rows[0:P:SQUARE, :].rearrange("g (q c) -> g q c", c=SQUARE),
+            b.rearrange("(q g c) o -> g q (c o)", q=BLOCKS, c=SQUARE),
+        )
         nc.sync.dma_start(plane2[:], w_rows[:, 2, :])
         nc.sync.dma_start(plane3[:], w_rows[:, 3, :])
         for c in range(PIECES):
             nc.sync.dma_start(x_raw[c][:], x_rows[:, :, c * C : (c + 1) * C])
-        turned = psum.tile([P, P], F32, name="turned", tag="bank")
-        nc.tensor.transpose(turned[:], b_rows[:], identity[:])
 
         picked01 = sbuf("picked01", [P, 2, S], F32)
         picked23 = sbuf("picked23", [P, 2, S], BF16)
@@ -113,10 +112,10 @@ def tile_picked_neuron_lin_relu_srt_e_kernel(tc, w, xT, b, offs, out):
             return acc[:]
 
         def finish_scalar(result, q, tokens):
-            nc.scalar.activation(result, multiply(q, tokens), RELU, bias=bias[:, q : q + 1])
+            nc.scalar.activation(result, multiply(q, tokens), RELU, bias=turned[:, q * SQUARE : q * SQUARE + 1])
 
         def finish_vector(result, q, tokens):
-            nc.vector.tensor_scalar(result, multiply(q, tokens), bias[:, q : q + 1], 0.0, op0=ADD, op1=MAX)
+            nc.vector.tensor_scalar(result, multiply(q, tokens), turned[:, q * SQUARE : q * SQUARE + 1], 0.0, op0=ADD, op1=MAX)
 
         def finish(c, first, finishers, blocks_a_store, slot=None):
             result = sbuf("result%d_%d" % (c, first), [P, len(finishers), C], F32, slot=slot)
@@ -129,7 +128,7 @@ def tile_picked_neuron_lin_relu_srt_e_kernel(tc, w, xT, b, offs, out):
 
         gather_vector(picked01[:, 0, :], planes01[:, 0, :], 0, S)
         gather_scalar(picked01[:, 1, :], planes01[:, 1, :], 0, S)
-        nc.scalar.copy(out=bias[:], in_=turned[:, 0:BLOCKS])
+        nc.vector.transpose(turned[:], b_rows[:])
         for q in range(BLOCKS):
             insert(q, 0, picked01)
         gather_vector(picked23[:, 0, 0 : 2 * P], plane2[:], 0, 2 * P)
@@ -137,12 +136,14 @@ def tile_picked_neuron_lin_relu_srt_e_kernel(tc, w, xT, b, offs, out):
 
         for q in range(BLOCKS):
             (gather_vector, gather_scalar)[q % 2](picked23[:, 1, q * P : (q + 1) * P], plane3[:], q * P, P)
-        for q in range(BLOCKS):
-            insert(q, 2, picked23)
+        insert(0, 2, picked23)
+        insert(1, 2, picked23)
+        quantise_w(0)
+        insert(2, 2, picked23)
+        insert(3, 2, picked23)
         weave_x(nc.scalar.copy, 0, slice(0, C))
         weave_x(nc.scalar.copy, 1, slice(0, C))
         weave_x(nc.scalar.copy, 2, slice(0, SHARE))
-        quantise_w(0)
         quantise_x(0)
         for q in range(1, BLOCKS):
             quantise_w(q)

@@ -154,7 +154,6 @@ def tile_picked_neuron_lin_relu_srt_e_kernel(tc, w, xT, b, offs, out):
         quantise_x(3)
 
         finish(0, 0, (finish_scalar,) * BLOCKS, 2, slot="x_raw1")
-        finish(1, 0, (finish_scalar, finish_scalar), 2)
-        finish(1, 2, (finish_vector, finish_scalar), 2, slot="x_woven2")
-        finish(2, 0, (finish_scalar, finish_vector) * 2, BLOCKS)
-        finish(3, 0, (finish_scalar, finish_vector) * 2, 2)
+        finish(1, 0, (finish_scalar,) * BLOCKS, 2)
+        finish(2, 0, (finish_vector, finish_scalar) * 2, BLOCKS)
+        finish(3, 0, (finish_vector, finish_scalar) * 2, 2)

@@ -154,6 +154,11 @@ def tile_picked_neuron_lin_relu_srt_e_kernel(tc, w, xT, b, offs, out):
         quantise_x(3)
 
         finish(0, 0, (finish_scalar,) * BLOCKS, 2, slot="x_raw1")
-        finish(1, 0, (finish_scalar,) * BLOCKS, 2)
-        finish(2, 0, (finish_vector, finish_scalar) * 2, BLOCKS)
+        last = BLOCKS - 1
+        finish(1, 0, (finish_scalar,) * last, last)
+        wide = sbuf("wide", [P, 2 * C], F32)
+        finish_scalar(wide[:, 0:C], last, slice(C, 2 * C))
+        finish_vector(wide[:, C : 2 * C], last, slice(2 * C, 3 * C))
+        nc.sync.dma_start(out_rows[:, last, C : 3 * C], wide[:])
+        finish(2, 0, (finish_scalar, finish_vector, finish_scalar), last)
         finish(3, 0, (finish_vector, finish_scalar) * 2, 2)

from contextlib import ExitStack

import concourse.mybir as mybir

K, N, T, S = 512, 2048, 512, 512
FLOPS = 2 * K * S * T

F32 = mybir.dt.float32
BF16 = mybir.dt.bfloat16
U32 = mybir.dt.uint32
U16 = mybir.dt.uint16
U8 = mybir.dt.uint8
FP8X4 = mybir.dt.float8_e4m3fn_x4
ADD, MAX = mybir.AluOpType.add, mybir.AluOpType.max
RELU = mybir.ActivationFunctionType.Relu
COPY = mybir.ActivationFunctionType.Copy

P = 128
PACK = 4
BLOCKS = S // P
C = 128
PIECES = T // C
ALIGN = 256
SHARE = 96
SQUARE = 32


def tile_picked_neuron_lin_relu_srt_e_kernel(tc, w, xT, b, offs, out):
    nc = tc.nc
    with ExitStack() as ctx:
        keep = ctx.enter_context(tc.tile_pool(name="keep", bufs=1))
        psum = ctx.enter_context(tc.psum_pool(name="psum", bufs=8))

        def sbuf(name, shape, dtype, slot=None):
            return keep.tile(shape, dtype, name=name, tag=slot or name, align_bytes=ALIGN)

        w_rows = w.rearrange("(p j) n -> p j n", j=PACK)
        x_rows = xT.rearrange("(p j) t -> p j t", j=PACK)
        out_rows = out.rearrange("(q p) t -> p q t", p=P)

        lists = sbuf("lists", [P, S // 16], U16)
        planes01 = sbuf("planes01", [P, 2, N], F32)
        plane2 = sbuf("plane2", [P, N], F32)
        plane3 = sbuf("plane3", [P, N], F32)
        x_raw = [sbuf("x_raw%d" % c, [P, PACK, C], F32) for c in range(PIECES)]
        b_rows = sbuf("b_rows", [P, P], F32)
        turned = sbuf("turned", [P, P], F32)

        nc.vector.memset(b_rows[:, 0 : P // 2], 0.0)
        nc.scalar.activation(b_rows[:, P // 2 : P], b_rows[:, 0 : P // 2], COPY)
        nc.sync.dma_start(planes01[:], w_rows[:, 0:2, :])
        nc.sync.dma_start(lists[:], offs)
        nc.sync.dma_start(
            b_rows[0:P:SQUARE, :].rearrange("g (q c) -> g q c", c=SQUARE),
            b.rearrange("(q g c) o -> g q (c o)", q=BLOCKS, c=SQUARE),
        )
        nc.sync.dma_start(plane2[:], w_rows[:, 2, :])
        nc.sync.dma_start(plane3[:], w_rows[:, 3, :])
        for c in range(PIECES):
            nc.sync.dma_start(x_raw[c][:], x_rows[:, :, c * C : (c + 1) * C])

        picked01 = sbuf("picked01", [P, 2, S], F32)
        picked23 = sbuf("picked23", [P, 2, S], BF16)
        w_woven = [sbuf("w_woven%d" % q, [P, P, PACK], BF16) for q in range(BLOCKS)]
        w_codes0 = sbuf("w_codes0", [P, P], U32)
        w_codes123 = sbuf("w_codes123", [P, BLOCKS - 1, P], U32, slot="x_raw0")
        w_codes = [w_codes0[:]] + [w_codes123[:, q, :] for q in range(BLOCKS - 1)]
        w_scales = [sbuf("w_scales%d" % q, [P, P], U8) for q in range(BLOCKS)]
        x_woven = [sbuf("x_woven%d" % c, [P, C, PACK], BF16) for c in range(PIECES)]
        x_codes = sbuf("x_codes", [P, T], U32)
        x_scales = sbuf("x_scales", [P, T], U8)

        def looked_up(window, first, count):
            return window.indirect(lists[:, first // 16 : (first + count) // 16])

        def gather_vector(picked, window, first, count):
            nc.vector.tensor_copy(picked, looked_up(window, first, count))

        def gather_scalar(picked, window, first, count):
            nc.scalar.activation(picked, looked_up(window, first, count), COPY)

        def insert(q, j, picked):
            nc.vector.tensor_copy(w_woven[q][:, :, j : j + 2], picked[:, :, q * P : (q + 1) * P].rearrange("p j n -> p n j"))

        def weave_x(copy, c, tokens):
            copy(
                out=x_woven[c][:, tokens, :].rearrange("p (c i) j -> p c j i", i=4),
                in_=x_raw[c][:, :, tokens].rearrange("p j (c i) -> p c j i", i=4),
            )

        def quantise(codes, scales, woven):
            nc.vector.quantize_mx(out=codes.bitcast(FP8X4), scales=scales, in_=woven.rearrange("p n j -> p (n j)"))

        def quantise_w(q):
            quantise(w_codes[q], w_scales[q][:], w_woven[q][:])

        def quantise_x(c):
            tokens = slice(c * C, (c + 1) * C)
            quantise(x_codes[:, tokens], x_scales[:, tokens], x_woven[c][:])

        def multiply(q, tokens):
            acc = psum.tile([P, tokens.stop - tokens.start], F32, name="acc", tag="bank")
            nc.tensor.matmul_mx(
                out=acc[:],
                lhsT=w_codes[q].bitcast(FP8X4),
                lhsT_scale=w_scales[q][:],
                rhs=x_codes[:, tokens].bitcast(FP8X4),
                rhs_scale=x_scales[:, tokens],
                start=True,
                stop=True,
            )
            return acc[:]

        def finish_scalar(result, q, tokens):
            nc.scalar.activation(result, multiply(q, tokens), RELU, bias=turned[:, q * SQUARE : q * SQUARE + 1])

        def finish_vector(result, q, tokens):
            nc.vector.tensor_scalar(result, multiply(q, tokens), turned[:, q * SQUARE : q * SQUARE + 1], 0.0, op0=ADD, op1=MAX)

        def finish(c, first, finishers, blocks_a_store, slot=None):
            result = sbuf("result%d_%d" % (c, first), [P, len(finishers), C], F32, slot=slot)
            tokens = slice(c * C, (c + 1) * C)
            for r, finisher in enumerate(finishers):
                finisher(result[:, r, :], first + r, tokens)
                if (r + 1) % blocks_a_store == 0:
                    low = r + 1 - blocks_a_store
                    nc.sync.dma_start(out_rows[:, first + low : first + r + 1, tokens], result[:, low : r + 1, :])

        gather_vector(picked01[:, 0, :], planes01[:, 0, :], 0, S)
        gather_scalar(picked01[:, 1, :], planes01[:, 1, :], 0, S)
        nc.vector.transpose(turned[:], b_rows[:])
        for q in range(BLOCKS):
            insert(q, 0, picked01)
        gather_vector(picked23[:, 0, 0 : 2 * P], plane2[:], 0, 2 * P)
        gather_scalar(picked23[:, 0, 2 * P : S], plane2[:], 2 * P, 2 * P)

        for q in range(BLOCKS):
            (gather_vector, gather_scalar)[q % 2](picked23[:, 1, q * P : (q + 1) * P], plane3[:], q * P, P)
        insert(0, 2, picked23)
        insert(1, 2, picked23)
        quantise_w(0)
        insert(2, 2, picked23)
        insert(3, 2, picked23)
        weave_x(nc.scalar.copy, 0, slice(0, C))
        weave_x(nc.scalar.copy, 1, slice(0, C))
        weave_x(nc.scalar.copy, 2, slice(0, SHARE))
        quantise_x(0)
        for q in range(1, BLOCKS):
            quantise_w(q)
        quantise_x(1)
        weave_x(nc.vector.tensor_copy, 2, slice(SHARE, C))
        weave_x(nc.vector.tensor_copy, 3, slice(0, C))
        quantise_x(2)
        quantise_x(3)

        finish(0, 0, (finish_scalar,) * BLOCKS, 2, slot="x_raw1")
        last = BLOCKS - 1
        finish(1, 0, (finish_scalar,) * last, last)
        wide = sbuf("wide", [P, 2 * C], F32)
        finish_scalar(wide[:, 0:C], last, slice(C, 2 * C))
        finish_vector(wide[:, C : 2 * C], last, slice(2 * C, 3 * C))
        nc.sync.dma_start(out_rows[:, last, C : 3 * C], wide[:])
        finish(2, 0, (finish_scalar, finish_vector, finish_scalar), last)
        finish(3, 0, (finish_vector, finish_scalar) * 2, 2)
